import numpy as np, ml_dtypes
CORES = [2,6,10,14,18,22,26,30]
N = 8
BF = ml_dtypes.bfloat16
W, L, B, V, S = 4096, 128, 4, 6, 2
def parts(rng):
    x = rng.integers(0, 256, (N, 8, 16, W))
    pool = rng.integers(0, W, (N, 8, 1, B, L, 6)); q = np.take_along_axis(pool, rng.integers(0, 6, (N, 8, 16, B, L, 2)), 5)
    q[..., 1] = np.where(rng.random((N, 8, 16, B, L)) < 0.5, q[..., 1], rng.integers(0, W, (N, 8, 16, B, L)))
    h = rng.integers(0, W, (N, 8, 16, L)); g = rng.integers(0, W, (N, 8, 16, L)); z = rng.integers(0, 256, (N, 8, 16, L))
    t = rng.choice(np.array([750, 900, 1050, 1200]), (N, 8, 1, 1)) + rng.integers(0, 300, (N, 8, 16, 1))
    return x, q, h, g, z, t
def pack(x, q, h, g, z, t):
    c = lambda a, n: np.ascontiguousarray(np.reshape(a, (N, 128, n))).astype(np.int32)
    return {"xt": c(x, W).astype(np.float32).astype(BF), "qs": c(q, 2 * B * L), "hn": c(h, L), "gt": c(g, L), "zs": c(z, L), "th": c(t, 1)}
def setup_inputs(rng):
    return pack(*parts(rng))
def setup_inputs_spread(rng):
    x, q, h, g, z, t = parts(rng); lg = W.bit_length() - 1
    x = np.minimum((np.exp2(8 * rng.random((N, 8, 1, W))) * rng.random((N, 8, 16, W))).astype(np.int64), 255)
    uneven = lambda *s: np.minimum(np.exp2(lg * rng.random(s)).astype(np.int64), W) - 1
    m = rng.random(q.shape) < 0.6; q = np.where(m, uneven(*q.shape), q); h = uneven(*h.shape); g = np.where(rng.random(g.shape) < 0.5, uneven(*g.shape), g)
    z = np.minimum((np.exp2(8 * rng.random((N, 8, 1, L))) * rng.random((N, 8, 16, L))).astype(np.int64), 255)
    t = np.where(rng.random((N, 8, 16, 1)) < 0.5, rng.integers(0, 4081, (N, 8, 16, 1)), rng.integers(200, 1200, (N, 8, 16, 1)))
    return pack(x, q, h, g, z, t)
def setup_inputs_ends(rng):
    two = lambda *s: rng.integers(0, 2, s)
    kind = rng.integers(0, 3, (N, 8, 1, W)); x = 255 * np.where(kind == 2, two(N, 8, 16, W), kind)
    odd = (np.arange(8) & 1)[None, :, None]; x[..., 0] = 255 * odd; x[..., W - 1] = 255 - 255 * odd
    q = (W - 1) * two(N, 8, 16, B, L, 2); h = (W - 1) * two(N, 8, 16, L); g = (W - 1) * two(N, 8, 16, L)
    kind = rng.integers(0, 3, (N, 8, 1, L)); z = 255 * np.where(kind == 2, two(N, 8, 16, L), kind); z[..., 0] = 0; z[..., L - 1] = 255
    t = 4080 * two(N, 8, 16, 1); t[:, 0::2, 0] = 0; t[:, 1::2, 0] = 4080; t[:, :, 2] = 4080; t[:, :, 15] = 4080
    for l in (0, 5, L - 1):
        for k in (2, 15):
            h[:, :, k, l] = W - 1; g[:, :, k, l] = 0; q[:, :, k, :, l] = 0
    return pack(x, q, h, g, z, t)
def setup_inputs_corners(rng):
    x, q, h, g, z, t = parts(rng); off = int(rng.integers(0, 6))
    for r in range(N):
        for a in range(8):
            o = rng.permutation(16); p = (r + a + off) % 6; e = np.zeros(16, np.int64)
            if p == 0: e[:] = 4080
            if p == 2: e[o[1:]] = 4080
            if p == 3: e[o[0]] = 4080
            if p == 4: e[0] = 4080; e[15] = 4080
            if p == 5: e = rng.choice(np.array([0, 1000, 1365, 4080]), 16)
            t[r, a, :, 0] = e
    q[:, :, :, :, 0::4] = 0; h[..., 0::4] = 0; g[..., 0::4] = 0
    q[:, :, :, :, 1::4] = rng.integers(0, W, (N, 8, 1, 1, len(range(1, L, 4)), 1))
    h[..., 2::4] = q[:, :, :, 0, 2::4, 0]; g[..., 2::4] = q[:, :, :, 0, 2::4, 1]
    z[..., 0:2] = 0; z[..., L - 2:] = 255
    return pack(x, q, h, g, z, t)
def setup_inputs_ties(rng):
    x, q, h, g, z, t = parts(rng)
    x = rng.integers(0, 253, (N, 8, 16, 1)) + rng.integers(0, 4, (N, 8, 16, W)) * (rng.random((N, 8, 16, W)) < 0.25)
    t = rng.integers(0, 10, (N, 8, 16, 1))
    return pack(x, q, h, g, z, t)
def setup_inputs_high(rng):
    x, q, h, g, z, t = parts(rng); near = lambda *s: rng.integers(W - 32, W, s)
    gap = rng.choice(np.array([130, 180, 252]), (N, 8, 1, 1))
    x = gap * rng.integers(0, 2, (N, 8, 1, W)) + rng.integers(0, 4, (N, 8, 16, W)) * (rng.random((N, 8, 16, W)) < 0.25)
    t = np.where(rng.random((N, 8, 16, 1)) < 0.25, rng.integers(0, 40, (N, 8, 16, 1)), 16 * gap + rng.integers(-12, 13, (N, 8, 16, 1)))
    d = rng.choice(np.array([3, 5]), (N, 8, 1, L)); one = np.arange(16)[:, None] == rng.integers(0, 16, (N, 8, 1, L))
    z = np.where(rng.random((N, 8, 1, L)) < 0.75, 255 - d * one, rng.integers(250, 256, (N, 8, 16, L)))
    tail = np.where(d == 5, W - 3, W - 5)[:, :, :, None]; name = np.where(d == 5, W - 21, W - 19)[:, :, :, None]
    q[..., 1] = np.where(rng.random((N, 8, 16, B, L)) < 0.75, tail, near(N, 8, 16, B, L))
    q[..., 0] = np.where(rng.random((N, 8, 16, B, L)) < 0.5, name, near(N, 8, 16, B, L))
    ab = np.array([[W - 5, W - 19], [W - 3, W - 21], [W - 19, W - 5], [W - 21, W - 3]])[rng.integers(0, 4, (N, 8, 16, L))]
    m = rng.random((N, 8, 16, L)) < 0.5; h = np.where(m, ab[..., 0], near(N, 8, 16, L)); g = np.where(m, ab[..., 1], near(N, 8, 16, L))
    return pack(x, q, h, g, z, t)
def check_inputs(d):
    bad = []
    for k, lo, hi in (("xt", 0, 255), ("qs", 0, W - 1), ("hn", 0, W - 1), ("gt", 0, W - 1), ("zs", 0, 255), ("th", 0, 4080)):
        v = np.asarray(d[k]).astype(np.float32)
        if not (np.min(v) >= lo and np.max(v) <= hi): bad.append("range of " + k)
        elif np.any(v != np.floor(v)): bad.append("whole numbers in " + k)
    return bad
def rec(x, a, b):
    ix = ((a * b >> 5) + a + 37 * b) & (W - 1)
    return np.take_along_axis(x, ix.reshape(N, 8, 1, 16 * L), 3).reshape(N, 8, 16, 16, L)
def reference(xt, qs, hn, gt, zs, th):
    x0 = xt.astype(np.float32).astype(np.int32).reshape(N, 8, 16, W); q = qs.astype(np.int64).reshape(N, 8, 16, B, L, 2)
    h = hn.astype(np.int64).reshape(N, 8, 16, L); g = gt.astype(np.int64).reshape(N, 8, 16, L); z = zs.astype(np.int64).reshape(N, 8, 16, L)
    lim = th.astype(np.int64).reshape(N, 8, 16, 1); cnt = np.zeros((N, 8, 1, L), np.int64); row = np.arange(16); prev = None
    for v in range(V):
        u = np.add.reduce(z, axis=2)[:, :, None]
        cal = u & (B - 1); rf = np.take_along_axis(q, cal[:, :, :, None, :, None], 3)[:, :, :, 0]
        R = rf[..., 0]; F = rf[..., 1]; x = rec(x0, h, g)
        usek = np.zeros((N, 8, 16, L), bool); usej = np.zeros((N, 8, 16, L), bool); mate = np.zeros((N, 8, 16, L), np.int64); top = np.full((N, 8, 16, L), -1, np.int64)
        for s in range(S):
            j = (row + 5 * s + v) & 15
            y = rec(x0, R[:, :, j], F[:, :, j]); dist = np.add.reduce(np.abs(x - y), axis=2)
            m = (dist < lim + cnt) & ~usek & ~usej[:, :, j]
            top = np.maximum(top, np.max(np.where(m[:, :, None], y, -1), axis=3))
            usek = usek | m; usej[:, :, j] = usej[:, :, j] | m; mate = np.where(m, j[None, None, :, None], mate)
            hit = np.any(m, axis=2)[:, :, None]; low = np.argmax(m, axis=2)[:, :, None]
            old = np.take_along_axis(R[:, :, j], low, 2); new = np.take_along_axis(h, low, 2)
            R = np.where(hit & (R == old), new, R); F = np.where(hit & (F == old), new, F)
        fj = np.take_along_axis(F, mate, 2); g = np.where(usek, ((fj * u >> 5) + fj) & (W - 1), g)
        if v > 0:
            Rb = np.roll(R, -1, axis=0); Fb = np.roll(F, -1, axis=0); ub = np.roll(usej, -1, axis=0)
            for b in range(B):
                put = (prev == b) & ~ub
                q[:, :, :, b, :, 0] = np.where(put, Rb, q[:, :, :, b, :, 0]); q[:, :, :, b, :, 1] = np.where(put, Fb, q[:, :, :, b, :, 1])
        cnt = np.add.reduce(usek.astype(np.int64), axis=2)[:, :, None]; z = np.where(cnt > 0, (z + top) >> 1, z); prev = cal
        if v < V - 1:
            h = np.roll(h, 1, axis=0); g = np.roll(g, 1, axis=0); z = np.roll(z, 1, axis=0); cnt = np.roll(cnt, 1, axis=0)
    return {"yq": q.reshape(N, 128, 2 * B * L).astype(np.float32), "yg": g.reshape(N, 128, L).astype(np.float32), "yz": z.reshape(N, 128, L).astype(np.float32)}

@@ -1,0 +1,661 @@
+from concourse.bass import DstId, RemoteDMATransfer
+from concourse.mybir import AluOpType as OP, ActivationFunctionType as AF
+
+NCH, L, NV, NP = 2, 64, 6, 4
+PL = L // NP
+XOFF = 8
+BIG = float(2 ** 25)
+MAGIC = float(3 * 2 ** 22)
+SIZE = {"fa": 4, "ba": 2, "ia": 4, "ua": 2}
+CY, PCY, HOP = 1.04e-3, 0.55e-3, 0.10
+GCY, SCY = 1.56, 3.8
+PLAN = (4.0, 0.6, 0.5, 'MGIKNFMMLMMZNMKMRNMVJKCJPRSJJMMNNMMMOMMKKJKPRNQLQMPMMQSMQKNJLOPMMQMJWOPUSQMRXQMMMMKZJOMMVLMMANMMSLMMJTKMJEONKTMPMMLMFMJMONDLIMJAMMMMMMMLJUMMMYNGNJNJMMPMMRLKKVMPMMLNLQRALJQOLMPQPRONMTZLCOPKDMLOPMYPJDNMOMJNMJNSJTMMPJMKMPOJMMMELNOJLYVMMJLPLTLMMKNIQSMRMAMVMHMWKOPLNFKOMMNIMLHOJGOJMHIVPPGPLPZJ')
+PRP = True
+N1D = True
+FUSE = False
+
+
+def sl(v, a, b, step=1):
+    return (v[0], v[1] + a, v[1] + b, step, v[4])
+
+
+def row(v):
+    return (v[0], v[1], v[2], v[3], 1)
+
+
+def count(v):
+    if v[0] == "ind":
+        return 16 * count(v[2])
+    return (v[2] - v[1] + v[3] - 1) // v[3]
+
+
+def isap(v):
+    return isinstance(v, tuple)
+
+
+def build():
+    top = {"fa": 0, "ba": 0, "ia": 0, "ua": 0}
+    ops, sems = [], []
+    lastgrp = {}
+    now = [0, -1]
+    slots, seen = {}, {}
+
+    def al(arena, n):
+        a = top[arena]
+        top[arena] = a + (n + 15) // 16 * 16
+        return (arena, a, a + n, 1, 128)
+
+    def spans(v):
+        if v[0] == "ind":
+            return spans(v[1]) + spans(v[2])
+        return [(v[0], v[1], v[2], v[3])]
+
+    def add(eng, kind, args, rd, wr, busy, lat=0.0, sem=None, extra=()):
+        r, w = [], []
+        for v in rd:
+            r += spans(v)
+        for v in wr:
+            if v[0] == "ind":
+                w += spans(v[1])
+                r += spans(v[2])
+            else:
+                w += spans(v)
+        banks = sorted(set(s[0] for s in r + w if s[0].startswith("ps")))
+        ops.append({"eng": eng, "kind": kind, "args": args, "r": r, "w": w, "busy": busy, "lat": lat, "sem": sem,
+                    "banks": banks, "extra": list(extra), "chunk": now[0], "visit": now[1],
+                    "slot": 0})
+        if now[1] >= 0 and eng != "R":
+            sig = (now[0], eng, kind, tuple(s[0] for s in w), tuple((s[0], s[2] - s[1]) for s in r))
+            seen[(now[1], sig)] = seen.get((now[1], sig), 0) + 1
+            ops[-1]["slot"] = slots.setdefault((sig, seen[(now[1], sig)]), len(slots) + 1)
+        return len(ops) - 1
+
+    def narrow(vs):
+        return all(v[0] in ("ba", "ua") for v in vs)
+
+    def vcost(out, ins, per):
+        if out[0] == "ind":
+            return 0.05 + count(out) * SCY * CY
+        if ins and ins[0][0] == "ind":
+            return 0.05 + count(out) * GCY * CY
+        return 0.03 + max(64, count(out) * per) * CY
+
+    def tt(out, a, b, op):
+        per = 1.0 if (a[0].startswith("ps") or b[0].startswith("ps")) else (1.0 if narrow([out, a, b]) else 2.0)
+        add("V", "tt", (out, a, b, op), [a, b], [out], vcost(out, [a], per))
+
+    def ts(out, a, s1, s2, op0, op1=None):
+        rd = [a] + [s for s in (s1, s2) if isap(s)]
+        add("V", "ts", (out, a, s1, s2, op0, op1), rd, [out], vcost(out, [a], 0.5 if narrow([out, a]) else 1.0))
+
+    def cp(out, a):
+        add("V", "cp", (out, a), [a], [out], vcost(out, [a], 0.5 if narrow([out, a]) else 1.0))
+
+    def ms(out, c):
+        add("V", "ms", (out, c), [], [out], vcost(out, [], 0.5 if narrow([out]) else 1.0))
+
+    def scan(out, d0, d1):
+        add("V", "scan", (out, d0, d1), [d0, d1], [out], vcost(out, [d0], 0.5))
+
+    def act(out, a, func, bias=0.0, scale=1.0):
+        rd = [a] + [s for s in (bias, scale) if isap(s)]
+        add("S", "act", (out, a, func, bias, scale), rd, [out], 0.065 + count(out) * (GCY if a[0] == "ind" else 1.0) * CY)
+
+    def mm(lst, ends="se"):
+        bank = lst[0][0][0]
+        group = lastgrp.get(bank, [])
+        busy = 0.03 + sum(max(64, count(m[2])) * (4 if m[2][0] == "fa" else 1) for m in lst) * PCY
+        i = add("P", "mm", (lst, "s" in ends, "e" in ends), [m[1] for m in lst] + [m[2] for m in lst], [m[0] for m in lst],
+                busy, 0.05, None, group if ends else group[:1])
+        lastgrp[bank] = [i] if "s" in ends else group + [i]
+
+    def iota(out, pattern, base, cm):
+        add("G", "iota", (out, pattern, base, cm), [], [out], 0.15 + 2 * count(out) * CY)
+
+    def dma(eng, out, a, lat):
+        s = "d%d" % len(sems)
+        sems.append(s)
+        add(eng, "dma", (out, a), [a] if a[0] != "hbm" else [], [out] if out[0] != "hbm" else [], 0.1, lat, s)
+
+    def send(items, lat):
+        full = []
+        for d, src, dst in items:
+            s = "r%d" % len(sems)
+            sems.append(s)
+            full.append((d, src, dst, s))
+        i = add("G", "send", full, [it[1] for it in full], [], 0.6)
+        for d, src, dst, s in full:
+            add("R", "arrive", (d, s), [], [dst], 0.0, lat, s, [i])
+
+    XW = al("ba", XOFF + 4096)
+    QI, HI, GI, ZI, TI = al("ia", 1024), al("ia", 128), al("ia", 128), al("ia", 128), al("ia", 1)
+    dma("S", HI, ("hbm", "hn"), 2.0)
+    dma("Y", GI, ("hbm", "gt"), 2.0)
+    dma("S", ZI, ("hbm", "zs"), 2.1)
+    dma("Y", QI, ("hbm", "qs"), 3.0)
+    dma("S", TI, ("hbm", "th"), 2.2)
+    dma("Y", sl(XW, XOFF, XOFF + 4096), ("hbm", "xt"), 5.5)
+
+    i1, i2, i3, i4, i5, i6 = al("ia", 128), al("ia", 128), al("ia", 128), al("ia", 144), al("ia", NV), al("ia", L // 8)
+    iota(i1, [[-1, 128]], 256, 1)
+    iota(i2, [[-16, 8], [0, 16]], 0, 1)
+    iota(i4, [[1, 144]], -14, 0)
+    iota(i5, [[-1, NV]], 16, 1)
+    iota(i6, [[16, L // 8]], 0, 0)
+    iota(i3, [[-1, 128]], 261, 1)
+    j1, j2, j3, j5 = al("ia", 128), al("ia", 128), al("ia", 128), al("ia", NV)
+    ONEb, DM, DM5, tmpb = al("ba", 128), al("ba", 128), al("ba", 128), al("ba", 128)
+    ts(j1, i1, 15, None, OP.bitwise_and)
+    ts(j2, i2, 4, None, OP.arith_shift_right)
+    ts(ONEb, j2, 0.0, None, OP.is_equal)
+    ts(tmpb, j2, 0.0, -64.0, OP.not_equal, OP.mult)
+    tt(DM, j1, tmpb, OP.add)
+    ts(j5, i5, 15, None, OP.bitwise_and)
+    KP, G16, IO = al("fa", NV), al("fa", 1), al("fa", L // 8)
+    cp(KP, j5)
+    ts(IO, i6, sl(KP, 0, 1), None, OP.add)
+    ts(G16, sl(i5, 0, 1), sl(KP, 0, 1), -16.0, OP.subtract, OP.add)
+    SEL, DG, C14 = al("ba", 144), al("ba", 144), al("ba", 144)
+    ts(C14, i4, G16, None, OP.subtract)
+    ts(SEL, C14, 1.0, -BIG, OP.is_equal, OP.mult)
+    t144 = al("ba", 144)
+    ts(t144, C14, 0.0, float(2 * L), OP.is_ge, OP.mult)
+    ts(DG, C14, 1.0, None, OP.is_le)
+    tt(DG, DG, t144, OP.mult)
+
+    def mat(arena, d, w):
+        m = al(arena, 128)
+        ts(m, DM, float(d), float(w), OP.is_equal, OP.mult)
+        return m
+
+    def scaled(arena, src, w):
+        m = al(arena, 128)
+        act(m, src, AF.Identity, 0.0, float(w))
+        return m
+
+    If, R5, R1 = mat("fa", 0, 1), mat("fa", 5, 1), mat("fa", 15, 1)
+    I32, I1184, nI = scaled("fa", If, 32), scaled("fa", If, 1184), scaled("fa", If, -1)
+    ONE = scaled("fa", ONEb, 1)
+    I8k = scaled("ba", If, 8192)
+    R5a, R5b, I25 = scaled("fa", R5, 32), scaled("fa", R5, 1184), scaled("ba", If, BIG)
+    ONE2k, nI32, Ihb, R1a = scaled("ba", ONEb, 2048), scaled("fa", If, -32), scaled("ba", If, 0.5), scaled("fa", R1, 32)
+    nONE128, Ib, nR1, nR5 = scaled("ba", ONEb, -128), scaled("ba", If, 1), scaled("fa", R1, -1), scaled("fa", R5, -1)
+    R11, R11u, R4, R10 = mat("ba", 11, 8192), mat("ba", 11, 1), mat("fa", 4, 1), mat("fa", 10, 1)
+    BK1 = scaled("ba", R11, -1)
+    BK0, BLK, b5, b0 = al("ba", 128), al("ba", 128), mat("ba", 5, 2 ** 38), mat("ba", 0, 2 ** 38)
+    tt(BK0, I8k, R11, OP.subtract)
+    tt(BLK, b5, b0, OP.subtract)
+    ts(j3, i3, 15, None, OP.bitwise_and)
+    tt(DM5, j3, tmpb, OP.add)
+    W, WR = [], []
+    for t in range(NV):
+        for lst, d, diag in ((W, DM, I8k), (WR, DM5, R11)):
+            m = al("ba", 128)
+            ts(m, d, sl(KP, t, t + 1), -8192.0, OP.is_gt, OP.mult)
+            tt(m, m, diag, OP.add)
+            lst.append(m)
+    ONES = al("ba", 2 * L)
+    ms(ONES, 1.0)
+    cb = {}
+    for c in (-51 * 2 ** 17, -2048, 32, -2 ** 23, 65536, -0.25, -1, -4096, 0):
+        cb[c] = al("ba", 128)
+        ms(cb[c], float(c))
+
+    def bias(out, c):
+        return (out, row(cb[c]), row(sl(ONES, 0, count(out))))
+
+    RS = al("ba", 16 * PL)
+    ms(RS, 1.0)
+    ms(sl(RS, 0, 16 * PL, 16), 0.0)
+    ms(sl(XW, 0, XOFF), 0.0)
+
+    ps = [("ps%d" % b, 0, 512, 1, 128) for b in range(8)]
+    TH = al("fa", 16 * NV)
+    H = [al("fa", 128) for t in range(NV)]
+    HN = [al("fa", 128) for t in range(NV)]
+    ts(sl(TH, 0, 1), TI, -0.5, BIG, OP.add, OP.mult)
+    cp(H[0], HI)
+
+    def turn(t):
+        pH, pT = sl(ps[0], 384, 512), sl(ps[3], 384, 385)
+        mm([(pH, R1, H[t])])
+        act(HN[t], pH, AF.Identity)
+        send([("f", HN[t], H[t + 1])], 3.0)
+        mm([(pT, R1, sl(TH, 16 * t, 16 * t + 1))])
+        act(sl(TH, 16 * t + 16, 16 * t + 17), pT, AF.Identity)
+
+    AND, SHR = OP.bitwise_and, OP.arith_shift_right
+    ch = []
+    for c in range(NCH):
+        now[0] = c
+        d = {"Q": al("fa", XOFF + 8 * L)}
+        for n in ("lf", "sf"):
+            d[n] = [al("fa", 3 * L) for t in range(NV + 1)]
+        for n in ("lb", "sb"):
+            d[n] = [al("fa", 3 * L) for t in range(NV)]
+        for n in ("lu", "su"):
+            d[n] = [al("ua", L + L // 8) for t in range(NV + 1)]
+        for n in ("RF", "RF1", "d", "eq", "e", "nb", "tmp"):
+            d[n] = al("fa", 2 * L)
+        for n in ("t", "thA", "N0m", "J", "s", "us", "um0", "um1", "dm", "tt0", "tt1", "t2"):
+            d[n] = al("fa", L)
+        for n in ("N0", "N1", "I0", "I1", "Ng", "G", "Nx"):
+            d[n] = al("ia", L)
+        d["w"], d["Ix"] = al("ia", L // 8), al("ia", L + L // 8)
+        for n in ("X", "D", "AB", "Y", "SC"):
+            d[n] = al("ba", 16 * L)
+        for n in ("nm0", "uk", "zb", "zr"):
+            d[n] = al("ba", L)
+        for n in ("u0", "u1", "um16"):
+            d[n] = al("ua", L)
+        ch.append(d)
+        for b in range(4):
+            cp(sl(d["Q"], XOFF + 2 * L * b, XOFF + 2 * L * (b + 1)), sl(QI, 256 * b + 2 * L * c, 256 * b + 2 * L * (c + 1)))
+        ms(sl(d["Q"], 0, XOFF), 0.0)
+        for t in range(1, NV - 1):
+            if FUSE:
+                ms(sl(d["sb"][t], 2 * L, 3 * L), 0.0)
+
+    def xindex(c, Hs, Gc):
+        d = ch[c]
+        pp, pk = sl(ps[4 * c + 1], 6 * L, 7 * L), sl(ps[4 * c + 1], 7 * L, 8 * L)
+        act(pp, sl(Hs, L * c, L * c + L), AF.Identity, 1184.0)
+        act(pk, sl(Hs, L * c, L * c + L), AF.Identity, -4259840.0, 2080.0)
+        tt(d["t2"], pp, Gc, OP.mult)
+        tt(d["Nx"], pk, d["t2"], OP.add)
+        ts(sl(d["Ix"], 0, L), d["Nx"], 5, 4095, SHR, AND)
+
+    def callee(c, U):
+        d = ch[c]
+        pc = sl(ps[4 * c + 2], 7 * L, 7 * L + L // 8)
+        mm([(pc, sl(DG, 14 - 2 * k, 142 - 2 * k), sl(d["zb"], k, L, 8)) for k in range(8)])
+        tt(d["w"], pc, IO, OP.add)
+        ts(sl(d["Ix"], L, L + L // 8), d["w"], 8 * L - 1, None, AND)
+        ts(U, d["Ix"], float(XOFF), None, OP.add)
+
+    def update(c, t):
+        d = ch[c]
+        B, win = sl(d["lb"][t], 0, 2 * L), ("ind", d["Q"], sl(d["lu"][t - 1], L, L + L // 8))
+        act(d["nb"], B, AF.Identity, 0.0, -1.0)
+        tt(d["tmp"], win, d["nb"], OP.min)
+        tt(win, d["tmp"], B, OP.max)
+
+    def distance(c, U, pe):
+        d = ch[c]
+        for k in range(NP):
+            a, b = 16 * PL * k, 16 * PL * (k + 1)
+            tt(sl(d["D"], a, b), ("ind", XW, sl(U, PL * k, PL * (k + 1))), sl(d["X"], a, b), OP.subtract)
+            act(sl(d["AB"], a, b), sl(d["D"], a, b), AF.Abs)
+        mm([(pe, sl(SEL, 15 - p, 143 - p), sl(d["AB"], p, 16 * L, 16)) for p in range(16)], "e")
+
+    def rename(c, RF, pf, sign, po, pd, halves):
+        d = ch[c]
+        e1, e2 = sl(d["e"], 0, L), sl(d["e"], L, 2 * L)
+        mm([bias(po, -1)], "s")
+        mm([bias(pd, -4096)], "s")
+        act(e1, sl(pf, 0, L), AF.Relu, -8191.0, sign)
+        act(e2, sl(pf, L, 2 * L), AF.Relu, -4096.0, sign)
+        mm([(po, ONE, e1)], "e")
+        mm([(pd, ONE, e2)], "e")
+        for h in halves:
+            tt(sl(d["eq"], h, 2 * L, 2), sl(RF, h, 2 * L, 2), po, OP.is_equal)
+        for h in halves:
+            tt(sl(d["d"], h, 2 * L, 2), sl(d["eq"], h, 2 * L, 2), pd, OP.mult)
+
+    for c in range(NCH):
+        now[0] = c
+        d = ch[c]
+        f0 = d["lf"][0]
+        ts(sl(f0, 0, L), sl(GI, L * c, L * c + L), -2048.0, None, OP.add)
+        cp(d["zb"], sl(ZI, L * c, L * c + L))
+        xindex(c, H[0], sl(f0, 0, L))
+        callee(c, d["lu"][0])
+        cp(sl(f0, L, 2 * L), sl(ZI, L * c, L * c + L))
+        ms(sl(f0, 2 * L, 3 * L), 0.0)
+
+    def visit(c, t):
+        d = ch[c]
+        pA, pB, pC, pD = ps[4 * c:4 * c + 4]
+        e0, e1, pu, pw, pF, pN = [sl(pA, k * L, k * L + L) for k in range(6)]
+        pf0, pf1, pN0, pg = sl(pB, 0, 2 * L), sl(pB, 2 * L, 4 * L), sl(pB, 4 * L, 5 * L), sl(pB, 5 * L, 6 * L)
+        po0, po1, pm1, pzz, pcnt, pm = [sl(pC, k * L, k * L + L) for k in range(6)]
+        pd0, pd1, pb, pr = sl(pD, 0, L), sl(pD, L, 2 * L), sl(pD, 2 * L, 4 * L), sl(pD, 4 * L, 6 * L)
+        zr = d["zr"]
+        dR, dF = sl(d["d"], 0, 2 * L, 2), sl(d["d"], 1, 2 * L, 2)
+        U, LF, SF, SU = d["lu"][t], d["lf"][t], d["sf"][t + 1], d["su"][t + 1]
+        Gc, Z, A = sl(LF, 0, L), sl(LF, L, 2 * L), sl(LF, 2 * L, 3 * L)
+        Hc = sl(H[t], L * c, L * c + L)
+        RF, RF1, nm0, uk = d["RF"], d["RF1"], d["nm0"], d["uk"]
+        R, F, Ra, Fa = sl(RF, 0, 2 * L, 2), sl(RF, 1, 2 * L, 2), sl(RF1, 0, 2 * L, 2), sl(RF1, 1, 2 * L, 2)
+        last = t == NV - 1
+        if t > 1:
+            update(c, t - 1)
+        act(RF, ("ind", d["Q"], sl(U, L, L + L // 8)), AF.Identity)
+        for k in range(NP):
+            act(sl(d["X"], 16 * PL * k, 16 * PL * (k + 1)), ("ind", XW, sl(U, PL * k, PL * (k + 1))), AF.Identity)
+        mm([bias(pN0, -51 * 2 ** 17)], "s")
+        mm([(pN0, I32, R), (pN0, I1184, F)], "e")
+        tt(d["t"], R, F, OP.mult)
+        tt(d["N0"], d["t"], pN0, OP.add)
+        ts(d["I0"], d["N0"], 5, 4095, SHR, AND)
+        ts(d["u0"], d["I0"], float(XOFF), None, OP.add)
+        act(d["thA"], A, AF.Identity, sl(TH, 16 * t, 16 * t + 1), BIG)
+        act(zr, Z, AF.Identity)
+        mm([bias(pu, 32), (pu, ONEb, zr)])
+        mm([bias(pw, -2 ** 23), (pw, ONE2k, zr), (pw, nI32, Gc)])
+        act(d["us"], pu, AF.Identity)
+        mm([(e0, If, d["thA"])], "s")
+        fa, fb = sl(pf0, 0, L), sl(pf0, L, 2 * L)
+        mm([bias(pf0, 0)], "s")
+        mm([(fa, nI, R)], "")
+        mm([(fb, nI, Hc)], "")
+        mm([(fb, If, R)], "")
+        if PRP:
+            mm([(pr, If, RF)])
+        distance(c, d["u0"], e0)
+        ts(nm0, e0, 0.0, -1.0, OP.is_gt, OP.mult)
+        mm([(fa, W[t], nm0), (fb, W[t], nm0)], "e")
+        mm([bias(pN, -51 * 2 ** 17), (pN, I25, nm0)], "s")
+        if N1D:
+            mm([(pN, R5a, R)], "")
+            mm([(pN, R5b, F)], "")
+        tt(d["N0m"], d["N0"], e0, OP.min)
+        tt(d["um0"], pu, nm0, OP.mult)
+        rename(c, RF, pf0, -1.0, po0, pd0, (0, 1))
+        tt(RF1, pr if PRP else RF, d["d"], OP.add)
+        tt(d["t"], Ra, Fa, OP.mult)
+        mm([(pN, R5a, dR if N1D else Ra)], "")
+        mm([(pN, R5b, dF if N1D else Fa)], "")
+        mm([(pN, R5, d["t"])], "e")
+        tt(d["N1"], pN, d["N0m"], OP.max)
+        ts(d["I1"], d["N1"], 5, 4095, SHR, AND)
+        ts(d["u1"], d["I1"], float(XOFF), None, OP.add)
+        ra, rb, rc, rd = (R5, R5a, nR5, R10) if last else (R1, R1a, nR1, R4)
+        fa, fb = sl(pf1, 0, L), sl(pf1, L, 2 * L)
+        mm([(e1, If, d["thA"]), (e1, BLK, nm0)], "s")
+        mm([bias(pf1, 0), (fb, If, Hc)], "s")
+        mm([(fa, If, Ra), (fa, WR[t], nm0)], "")
+        mm([(fb, nR5, Ra), (fb, W[t], nm0)], "")
+        mm([(pm1, R11u, nm0)], "s")
+        if t > 0:
+            mm([(pb, If, RF1)], "s")
+            mm([(sl(pb, h, 2 * L, 2), BK0, nm0) for h in range(2)], "")
+        distance(c, d["u1"], e1)
+        ts(uk, e1, 0.0, None, OP.is_gt)
+        mm([(fa, WR[t], uk), (fb, W[t], uk)], "e")
+        tt(d["J"], d["I1"], e1, OP.min)
+        ts(d["um16"], d["J"], float(-XOFF), float(XOFF), OP.max, OP.add)
+        mm([(pm1, R11u, uk)], "e")
+        if t > 0:
+            mm([(sl(pb, h, 2 * L, 2), BK1, uk) for h in range(2)], "e")
+        mm([bias(pF, -2048), (pF, If, Fa)], "s")
+        mm([bias(pg, 65536), (pg, rb, Gc)], "s")
+        tt(d["um1"], pm1, d["us"], OP.mult)
+        tt(d["dm"], pw, uk, OP.mult)
+        mm([(pg, ra, d["dm"])], "")
+        rename(c, RF1, pf1, 1.0, po1, pd1, (1, 0) if t > 0 else (1,))
+        mm([(pzz, Ib, zr), (pzz, nONE128, uk)])
+        if not last:
+            mm([(pcnt, ONEb, uk)])
+            act(sl(SF, 2 * L, 3 * L), pcnt, AF.Identity)
+        mm([(pF, If, dF)], "e")
+        tt(d["tt0"], pF, d["um0"], OP.mult)
+        tt(d["tt1"], pF, d["um1"], OP.mult)
+        mm([(pg, rc, d["tt0"])], "")
+        mm([(pg, rd, d["tt1"])], "e")
+        cp(d["Ng"], pg)
+        ts(d["G"], d["Ng"], 5, 4095, SHR, AND)
+        ts(sl(SF, 0, L), d["G"], 0.0 if last else -2048.0, None, OP.add)
+        if not last:
+            xindex(c, HN[t], sl(SF, 0, L))
+        if t > 0:
+            tt(sl(d["sb"][t], 0, 2 * L), pb, d["d"], OP.add)
+        for k in range(NP):
+            a, b = 16 * PL * k, 16 * PL * (k + 1)
+            act(sl(d["Y"], a, b), ("ind", XW, sl(d["um16"], PL * k, PL * (k + 1))), AF.Identity)
+            scan(sl(d["SC"], a, b), RS, sl(d["Y"], a, b))
+        mm([bias(pm, -0.25), (pm, Ihb, zr), (pm, Ihb, sl(d["SC"], 15, 16 * L, 16))])
+        ts(d["s"], pm, MAGIC, -MAGIC, OP.add, OP.add)
+        tt(d["zb"], d["s"], pzz, OP.max)
+        act(sl(SF, L, 2 * L), d["zb"], AF.Identity)
+        back = ("b", sl(d["sb"][t], 0, 2 * L), sl(d["lb"][t], 0, 2 * L))
+        if last:
+            send([back], 2.5)
+            dma("Y", ("hbm", "yg", L * c, L * c + L), sl(SF, 0, L), 2.0)
+            dma("Y", ("hbm", "yz", L * c, L * c + L), sl(SF, L, 2 * L), 2.0)
+            update(c, t)
+            for b in range(4):
+                dma("YS"[b % 2], ("hbm", "yq", 256 * b + 2 * L * c, 256 * b + 2 * L * (c + 1)),
+                    sl(d["Q"], XOFF + 2 * L * b, XOFF + 2 * L * (b + 1)), 2.2)
+        else:
+            callee(c, SU)
+            if FUSE and t > 0:
+                send([("f", SF, d["lf"][t + 1]), ("b", d["sb"][t], d["lb"][t])], 2.8)
+            else:
+                if t > 0:
+                    send([back], 2.5)
+                send([("f", SF, d["lf"][t + 1])], 2.8)
+            send([("f", SU, d["lu"][t + 1])], 2.2)
+
+    for t in range(NV):
+        now[1] = t
+        if t < NV - 1:
+            now[0] = 0
+            turn(t)
+        for c in range(NCH):
+            now[0] = c
+            visit(c, t)
+    return ops, sems, top
+
+
+def depend(ops):
+    hist = {}
+    for i, o in enumerate(ops):
+        hard, soft = set(), set()
+        for j in o["extra"]:
+            (hard if o["eng"] == "R" else soft).add(j)
+        for kind, sp in (("r", o["r"]), ("w", o["w"])):
+            for name, a, b, st in sp:
+                for j, k2, a2, b2, st2 in hist.get(name, []):
+                    if j != i and a < b2 and a2 < b and (kind == "w" or k2 == "w") and (st != st2 or (a - a2) % st == 0):
+                        if ops[j]["eng"] == "P" and o["eng"] == "P":
+                            soft.add(j)
+                        else:
+                            hard.add(j)
+        for name, a, b, st in o["w"]:
+            hist[name] = [h for h in hist.get(name, [])
+                          if not (a <= h[2] and h[3] <= b and (st == 1 or (st == h[4] and (a - h[2]) % st == 0)))]
+        for kind, sp in (("r", o["r"]), ("w", o["w"])):
+            for name, a, b, st in sp:
+                hist.setdefault(name, []).append((i, kind, a, b, st))
+        o["data"], o["soft"] = hard, soft - hard
+
+
+def schedule(ops, lead, look, step, shift):
+    n = len(ops)
+    for o in ops:
+        o["hard"] = set(o["data"])
+    succ = [[] for i in range(n)]
+    left = [0] * n
+    for i, o in enumerate(ops):
+        for j in o["hard"] | o["soft"]:
+            succ[j].append(i)
+            left[i] += 1
+    prio = [0.0] * n
+    for i in range(n - 1, -1, -1):
+        o = ops[i]
+        best = o["lat"]
+        for s in succ[i]:
+            best = max(best, prio[s] + (o["lat"] + HOP if i in ops[s]["hard"] else 0.0))
+        prio[i] = best + o["busy"]
+    for i in range(n):
+        k = ops[i]["slot"]
+        prio[i] += (lead if ops[i]["chunk"] == 0 else 0.0) + (step * (ord(shift[k]) - 77) if k < len(shift) else 0.0)
+    free, bank, done, order = {}, {}, [0.0] * n, []
+    ready = [i for i in range(n) if left[i] == 0]
+
+    def start(i):
+        o = ops[i]
+        s = free.get(o["eng"], 0.0) if o["eng"] != "R" else 0.0
+        for j in o["hard"]:
+            s = max(s, done[j] + HOP)
+        for b in o["banks"]:
+            for e, j in bank.get(b, {}).items():
+                if e != o["eng"]:
+                    s = max(s, done[j] + HOP)
+        return s
+
+    while ready:
+        st = [(start(i), i) for i in ready]
+        s0, i0 = min(st)
+        cand = [(prio[i], -i, s) for s, i in st if ops[i]["eng"] == ops[i0]["eng"] and s <= s0 + look * ops[i0]["busy"]]
+        p, i, s = max(cand)
+        i = -i
+        o = ops[i]
+        for b in o["banks"]:
+            for e, j in bank.get(b, {}).items():
+                if e != o["eng"]:
+                    o["hard"].add(j)
+            bank.setdefault(b, {})[o["eng"]] = i
+        o["start"] = s
+        free[o["eng"]] = s + o["busy"]
+        done[i] = s + o["busy"] + o["lat"]
+        order.append(i)
+        ready.remove(i)
+        for k in succ[i]:
+            left[k] -= 1
+            if left[k] == 0:
+                ready.append(k)
+    need = set()
+    for o in ops:
+        need |= o["hard"]
+    cnt = {}
+    for i in order:
+        o = ops[i]
+        o["inc"] = None
+        if o["sem"] is None and o["kind"] != "send" and i in need:
+            cnt[o["eng"]] = cnt.get(o["eng"], 0) + 1
+            o["inc"] = cnt[o["eng"]]
+    return order, cnt, max(done)
+
+
+OPS, SEMS, TOP = build()
+depend(OPS)
+ORDER, TOTAL, SPAN = schedule(OPS, *PLAN)
+
+SCRATCH = {"fa": ("sbuf", [128, TOP["fa"]], "float32"), "ba": ("sbuf", [128, TOP["ba"]], "bfloat16"),
+           "ia": ("sbuf", [128, TOP["ia"]], "int32"), "ua": ("sbuf", [128, TOP["ua"]], "uint16")}
+for _b in range(8):
+    SCRATCH["ps%d" % _b] = ("psum", [128, 512], "float32")
+SEMAPHORES = ["qV", "qS", "qP", "qG", "sent"] + SEMS
+
+
+def engines_of(T, topo, r):
+    n = len(T.cores)
+    e = {"f": topo.engines(T.cores[r], T.cores[(r + 1) % n]), "b": topo.engines(T.cores[r], T.cores[(r - 1) % n])}
+    small, large = ("f", "b") if len(e["f"]) <= len(e["b"]) else ("b", "f")
+    rest = [x for x in e[large] if x not in e[small]]
+    if not rest:
+        h = len(e[small]) // 2
+        e[small], rest = e[small][:h], e[small][h:]
+    e[large] = rest
+    for k in e:
+        m = 1
+        while 2 * m <= len(e[k]):
+            m *= 2
+        e[k] = e[k][:m]
+    return e
+
+
+def rank_program(g, core, T, topo):
+    r = T.rank_of(core)
+    if r is None:
+        return
+    n = len(T.cores)
+    mine = engines_of(T, topo, r)
+    dest = {"f": T.cores[(r + 1) % n], "b": T.cores[(r - 1) % n]}
+    comes = {"f": len(engines_of(T, topo, (r - 1) % n)["f"]), "b": len(engines_of(T, topo, (r + 1) % n)["b"])}
+    queue = {"V": g.vector, "S": g.scalar, "P": g.tensor, "G": g, "Y": g.sync}
+    seen = {e: {} for e in queue}
+    final = {}
+    sent = [0]
+
+    def ap(v):
+        if not isap(v):
+            return v
+        if v[0] == "ind":
+            return ap(v[1]).indirect(ap(v[2]))
+        if v[0] == "hbm":
+            return T[v[1]][:] if len(v) == 2 else T[v[1]][:, v[2]:v[3]]
+        cols = slice(v[1], v[2]) if v[3] == 1 else slice(v[1], v[2], v[3])
+        return T[v[0]][:, cols] if v[4] == 128 else T[v[0]][0:v[4], cols]
+
+    def mask(d):
+        return sum(1 << e for e in mine[d])
+
+    for i in ORDER:
+        o = OPS[i]
+        e, k, a = o["eng"], o["kind"], o["args"]
+        if e == "R":
+            final[a[1]] = comes[a[0]]
+            continue
+        q = queue[e]
+        want = {}
+        for j in o["hard"]:
+            p = OPS[j]
+            if p["eng"] == "R":
+                s, v = p["sem"], comes[p["args"][0]]
+            elif p["kind"] == "dma":
+                s, v = p["sem"], 16
+            else:
+                s, v = "q" + p["eng"], p["inc"]
+            want[s] = max(want.get(s, 0), v)
+        for s in sorted(want):
+            if seen[e].get(s, 0) < want[s]:
+                q.wait_ge(T.sem[s], want[s])
+                seen[e][s] = want[s]
+        if k == "tt":
+            ins = q.tensor_tensor(ap(a[0]), ap(a[1]), ap(a[2]), a[3])
+        elif k == "ts":
+            if a[5] is None:
+                ins = q.tensor_scalar(ap(a[0]), ap(a[1]), ap(a[2]), None, a[4])
+            else:
+                ins = q.tensor_scalar(ap(a[0]), ap(a[1]), ap(a[2]), ap(a[3]), a[4], a[5])
+        elif k == "cp":
+            ins = q.tensor_copy(ap(a[0]), ap(a[1]))
+        elif k == "ms":
+            ins = q.memset(ap(a[0]), a[1])
+        elif k == "scan":
+            ins = q.tensor_tensor_scan(ap(a[0]), ap(a[1]), ap(a[2]), 0.0, OP.mult, OP.max)
+        elif k == "act":
+            ins = q.activation(ap(a[0]), ap(a[1]), a[2], bias=ap(a[3]), scale=ap(a[4]))
+        elif k == "iota":
+            ins = q.iota(ap(a[0]), a[1], a[2], a[3])
+        elif k == "mm":
+            for m, (x, w, y) in enumerate(a[0]):
+                ins = q.matmul(ap(x), ap(w), ap(y), a[1] and m == 0, a[2] and m == len(a[0]) - 1)
+        elif k == "dma":
+            q.dma_start(ap(a[0]), ap(a[1])).then_inc(T.sem[o["sem"]], 16)
+            final[o["sem"]] = 16
+            continue
+        else:
+            if len(a) == 1:
+                d, src, dst, s = a[0]
+                rid, pid, se = topo.addr(dest[d])
+                g.remote_dma(ap(dst), ap(src), T.sem[s], T.sem.sent, pid, rid, mask(d))
+            else:
+                trs = []
+                for d, src, dst, s in a:
+                    rid, pid, se = topo.addr(dest[d])
+                    trs.append(RemoteDMATransfer(dst_ids=[DstId(rid=rid, pnc=pid)], dma_engine_mask=mask(d),
+                                                 remote_sem=T.sem[s], src=ap(src), dst=ap(dst)))
+                g.remote_dma_fused(trs, local_sem=T.sem.sent)
+            sent[0] += sum(len(mine[it[0]]) for it in a)
+            continue
+        if o["inc"] is not None:
+            ins.then_inc(T.sem["q" + e], 1)
+    for e in TOTAL:
+        final["q" + e] = TOTAL[e]
+    final["sent"] = sent[0]
+    for s in final:
+        g.wait_ge(T.sem[s], final[s])

@@ -1,26 +1,27 @@
+import math
 from concourse.bass import DstId, RemoteDMATransfer
 from concourse.mybir import AluOpType as OP, ActivationFunctionType as AF
 
-NCH, L, NV, NP = 2, 64, 6, 4
-PL = L // NP
-XOFF = 8
-BIG = float(2 ** 25)
-MAGIC = float(3 * 2 ** 22)
-SIZE = {"fa": 4, "ba": 2, "ia": 4, "ua": 2}
-CY, PCY, HOP = 1.04e-3, 0.55e-3, 0.10
-GCY, SCY = 1.56, 3.8
-PLAN = (4.0, 0.6, 0.5, 'MGIKNFMMLMMZNMKMRNMVJKCJPRSJJMMNNMMMOMMKKJKPRNQLQMPMMQSMQKNJLOPMMQMJWOPUSQMRXQMMMMKZJOMMVLMMANMMSLMMJTKMJEONKTMPMMLMFMJMONDLIMJAMMMMMMMLJUMMMYNGNJNJMMPMMRLKKVMPMMLNLQRALJQOLMPQPRONMTZLCOPKDMLOPMYPJDNMOMJNMJNSJTMMPJMKMPOJMMMELNOJLYVMMJLPLTLMMKNIQSMRMAMVMHMWKOPLNFKOMMNIMLHOJGOJMHIVPPGPLPZJ')
-PRP = True
-N1D = True
-FUSE = False
+NCH, L, NV, NB = 2, 64, 6, 4
+ZOFF = 1536.0
+CY, PCY, HOP = 1.0e-3, 0.52e-3, 0.16
+GCY, SCY, SEND = 1.56, 3.8, 0.8
+SHIFT = {'P bank0 448 1': 5.5, 'V SC 256 1': -6.0, 'S Fs 0 1': -3.8, 'S X 0 1': -1.8, 'V su 0 1': -3.6, 'P bank1 192 1': -7.8, 'V AB 768 1': -0.7, 'S AB 0 2': -1.0, 'S sb 128 1': -3.3, 'V D 512 1': -3.7, 'V dm 0 1': -0.5, 'V SC 0 1': 5.9, 'P bank2 256 2': -3.4, 'S m0 0 1': 0.9, 'S D 768 1': 4.9, 'P bank3 64 2': 2.0, 'V sb 0 1': 2.1, 'V SC 512 1': 0.5, 'V D 0 1': 1.5, 'V tmp 0 1': 0.7, 'Y zo 0 1': 5.1, 'P bank1 128 2': 3.1, 'V eq 0 1': 2.4, 'V S3 0 1': 1.9, 'S X 512 1': -0.7, 'G st 0 1': -0.4, 'P bank0 128 1': 0.1, 'S AB 512 2': 0.4, 'S AB 256 1': -0.8, 'P bank0 192 1': -0.6, 'P bank1 448 1': -1.8, 'V d 0 1': 2.2, 'S AB 256 3': 0.1, 'S e 0 2': 1.3, 'S X 256 1': 0.4, 'V QO 0 1': -0.8, 'V tmp 0 2': -0.4, 'S st 192 1': -0.3, 'V w 0 1': 0.3, 'V eq 1 1': -0.2, 'V t0 0 1': 1.0, 'S RF 0 1': -0.3, 'V D 256 2': 0.1, 'V t1 0 1': -1.7, 'V N0m 0 1': -0.1, 'V Ng 0 1': -0.3, 'R lu 0 1': 0.6, 'S AB 256 2': 1.3, 'P bank1 128 1': -1.6, 'V st 0 1': -0.2}
+CFG = {"lead": 4.1, "look": 0.3, "shift": SHIFT, "split": True,
+       "xp": (16, 16, 16, 16), "p0": (16, 16, 16, 16), "p1": (16, 16, 16, 16), "ps": (16, 16, 16, 16), "onv": ((3,), (3,)),
+       "xonv": ((), ()), "plain0": ((), ()), "plain1": ((3,), (3,)),
+       "banks": {"pN0": (1, 0), "e0": (3, 0), "pf0": (0, 0, 2), "po0": (1, 1), "p4": (2, 0, 4), "pN": (1, 2),
+                 "pF": (0, 2), "pH": (0, 3), "e1": (3, 1), "pf1": (0, 0, 2), "po1": (1, 1), "p3": (2, 4, 3),
+                 "pM": (0, 4, 2), "pwk": (0, 6), "pzr": (0, 7), "pb": (1, 3, 2), "pw": (1, 5), "pz": (3, 2),
+                 "pc": (3, 3), "pp": (1, 6), "pk": (1, 7)}}
 
 
 def sl(v, a, b, step=1):
     return (v[0], v[1] + a, v[1] + b, step, v[4])
 
 
-def row(v):
-    return (v[0], v[1], v[2], v[3], 1)
+def rows(v, n):
+    return (v[0], v[1], v[2], v[3], n)
 
 
 def count(v):
@@ -33,12 +34,19 @@ def isap(v):
     return isinstance(v, tuple)
 
 
-def build():
-    top = {"fa": 0, "ba": 0, "ia": 0, "ua": 0}
+def cuts(sizes):
+    out, a = [], 0
+    for s in sizes:
+        out.append((a, a + s))
+        a += s
+    return out
+
+
+def build(cfg):
+    top = {"fa": 0, "ba": 0, "ha": 0, "ia": 0, "ua": 0}
     ops, sems = [], []
-    lastgrp = {}
+    opened, named, seen = {}, {}, {}
     now = [0, -1]
-    slots, seen = {}, {}
 
     def al(arena, n):
         a = top[arena]
@@ -62,16 +70,20 @@ def build():
                 w += spans(v)
         banks = sorted(set(s[0] for s in r + w if s[0].startswith("ps")))
         ops.append({"eng": eng, "kind": kind, "args": args, "r": r, "w": w, "busy": busy, "lat": lat, "sem": sem,
-                    "banks": banks, "extra": list(extra), "chunk": now[0], "visit": now[1],
-                    "slot": 0})
-        if now[1] >= 0 and eng != "R":
-            sig = (now[0], eng, kind, tuple(s[0] for s in w), tuple((s[0], s[2] - s[1]) for s in r))
-            seen[(now[1], sig)] = seen.get((now[1], sig), 0) + 1
-            ops[-1]["slot"] = slots.setdefault((sig, seen[(now[1], sig)]), len(slots) + 1)
+                    "banks": banks, "extra": list(extra), "chunk": now[0], "visit": now[1], "group": None, "slot": None})
+        if now[1] >= 0:
+            name, a, b, st = (w + r)[0] if kind != "dma" else r[0]
+            for a0, b0, n in named.get(name, []):
+                if a0 <= a < b0:
+                    name, a = n, a - a0
+                    break
+            sig = (eng, name, a)
+            seen[(now[0], now[1], sig)] = seen.get((now[0], now[1], sig), 0) + 1
+            ops[-1]["slot"] = sig + (seen[(now[0], now[1], sig)],)
         return len(ops) - 1
 
     def narrow(vs):
-        return all(v[0] in ("ba", "ua") for v in vs)
+        return all(v[0] in ("ba", "ha", "ua") for v in vs)
 
     def vcost(out, ins, per):
         if out[0] == "ind":
@@ -81,87 +93,92 @@ def build():
         return 0.03 + max(64, count(out) * per) * CY
 
     def tt(out, a, b, op):
-        per = 1.0 if (a[0].startswith("ps") or b[0].startswith("ps")) else (1.0 if narrow([out, a, b]) else 2.0)
-        add("V", "tt", (out, a, b, op), [a, b], [out], vcost(out, [a], per))
+        per = 1.0 if (a[0].startswith("ps") or b[0].startswith("ps")) else 2.0
+        return add("V", "tt", (out, a, b, op), [a, b], [out], vcost(out, [a], per))
 
     def ts(out, a, s1, s2, op0, op1=None):
         rd = [a] + [s for s in (s1, s2) if isap(s)]
-        add("V", "ts", (out, a, s1, s2, op0, op1), rd, [out], vcost(out, [a], 0.5 if narrow([out, a]) else 1.0))
+        return add("V", "ts", (out, a, s1, s2, op0, op1), rd, [out], vcost(out, [a], 0.5 if narrow([out, a]) else 1.0))
 
     def cp(out, a):
-        add("V", "cp", (out, a), [a], [out], vcost(out, [a], 0.5 if narrow([out, a]) else 1.0))
+        return add("V", "cp", (out, a), [a], [out], vcost(out, [a], 0.5 if narrow([out, a]) else 1.0))
 
     def ms(out, c):
-        add("V", "ms", (out, c), [], [out], vcost(out, [], 0.5 if narrow([out]) else 1.0))
+        return add("V", "ms", (out, c), [], [out], vcost(out, [], 0.5 if narrow([out]) else 1.0))
 
-    def scan(out, d0, d1):
-        add("V", "scan", (out, d0, d1), [d0, d1], [out], vcost(out, [d0], 0.5))
+    def scan(out, d0, d1, op):
+        return add("V", "scan", (out, d0, d1, op), [d0, d1], [out], vcost(out, [d0], 0.5 if narrow([out, d0, d1]) else 1.0))
 
     def act(out, a, func, bias=0.0, scale=1.0):
         rd = [a] + [s for s in (bias, scale) if isap(s)]
-        add("S", "act", (out, a, func, bias, scale), rd, [out], 0.065 + count(out) * (GCY if a[0] == "ind" else 1.0) * CY)
+        return add("S", "act", (out, a, func, bias, scale), rd, [out],
+                   0.065 + count(out) * (GCY if a[0] == "ind" else 1.0) * CY)
 
-    def mm(lst, ends="se"):
-        bank = lst[0][0][0]
-        group = lastgrp.get(bank, [])
+    def mm(lst, ends="se", after=()):
+        key = lst[0][0][0]
+        group = [] if "s" in ends else opened[key]
         busy = 0.03 + sum(max(64, count(m[2])) * (4 if m[2][0] == "fa" else 1) for m in lst) * PCY
         i = add("P", "mm", (lst, "s" in ends, "e" in ends), [m[1] for m in lst] + [m[2] for m in lst], [m[0] for m in lst],
-                busy, 0.05, None, group if ends else group[:1])
-        lastgrp[bank] = [i] if "s" in ends else group + [i]
+                busy, 0.05, None, list(after) + (group if "e" in ends else group[:1]))
+        opened[key] = group + [i]
+        ops[i]["group"] = opened[key][0]
+        return i
 
     def iota(out, pattern, base, cm):
         add("G", "iota", (out, pattern, base, cm), [], [out], 0.15 + 2 * count(out) * CY)
+
+    def select(out, a, pattern, op, fill, base, cm):
+        add("G", "sel", (out, a, pattern, op, fill, base, cm), [a], [out], 0.2 + 2 * count(out) * CY)
 
     def dma(eng, out, a, lat):
         s = "d%d" % len(sems)
         sems.append(s)
         add(eng, "dma", (out, a), [a] if a[0] != "hbm" else [], [out] if out[0] != "hbm" else [], 0.1, lat, s)
 
-    def send(items, lat):
-        full = []
-        for d, src, dst in items:
-            s = "r%d" % len(sems)
-            sems.append(s)
-            full.append((d, src, dst, s))
-        i = add("G", "send", full, [it[1] for it in full], [], 0.6)
-        for d, src, dst, s in full:
-            add("R", "arrive", (d, s), [], [dst], 0.0, lat, s, [i])
+    def send(d, src, dst, lat, after=()):
+        s = "r%d" % len(sems)
+        sems.append(s)
+        i = add("G", "send", [(d, src, dst, s)], [src], [], SEND, extra=after)
+        add("R", "arrive", (d, s), [], [dst], 0.0, lat - HOP, s, [i])
+        return i
 
-    XW = al("ba", XOFF + 4096)
+    XW0 = al("ba", 16 + 4096)
+    XW = sl(XW0, 16, 16 + 4096)
     QI, HI, GI, ZI, TI = al("ia", 1024), al("ia", 128), al("ia", 128), al("ia", 128), al("ia", 1)
     dma("S", HI, ("hbm", "hn"), 2.0)
     dma("Y", GI, ("hbm", "gt"), 2.0)
     dma("S", ZI, ("hbm", "zs"), 2.1)
     dma("Y", QI, ("hbm", "qs"), 3.0)
     dma("S", TI, ("hbm", "th"), 2.2)
-    dma("Y", sl(XW, XOFF, XOFF + 4096), ("hbm", "xt"), 5.5)
+    dma("Y", XW, ("hbm", "xt"), 5.5)
 
-    i1, i2, i3, i4, i5, i6 = al("ia", 128), al("ia", 128), al("ia", 128), al("ia", 144), al("ia", NV), al("ia", L // 8)
+    AND, SHR = OP.bitwise_and, OP.arith_shift_right
+    K = 2.0 ** 25
+    i1, i2, i4, i5, i6 = al("ia", 128), al("ia", 128), al("ia", 144), al("ia", NV), al("ia", L // 8)
     iota(i1, [[-1, 128]], 256, 1)
     iota(i2, [[-16, 8], [0, 16]], 0, 1)
-    iota(i4, [[1, 144]], -14, 0)
     iota(i5, [[-1, NV]], 16, 1)
+    iota(i4, [[1, 144]], -14, 0)
     iota(i6, [[16, L // 8]], 0, 0)
-    iota(i3, [[-1, 128]], 261, 1)
-    j1, j2, j3, j5 = al("ia", 128), al("ia", 128), al("ia", 128), al("ia", NV)
-    ONEb, DM, DM5, tmpb = al("ba", 128), al("ba", 128), al("ba", 128), al("ba", 128)
-    ts(j1, i1, 15, None, OP.bitwise_and)
-    ts(j2, i2, 4, None, OP.arith_shift_right)
-    ts(ONEb, j2, 0.0, None, OP.is_equal)
+    j1, j2, j5 = al("ia", 128), al("ia", 128), al("ia", NV)
+    ONE, DM, tmpb = al("ba", 128), al("ba", 128), al("ba", 128)
+    ts(j1, i1, 15, None, AND)
+    ts(j2, i2, 4, None, SHR)
+    ts(ONE, j2, 0.0, None, OP.is_equal)
     ts(tmpb, j2, 0.0, -64.0, OP.not_equal, OP.mult)
     tt(DM, j1, tmpb, OP.add)
-    ts(j5, i5, 15, None, OP.bitwise_and)
-    KP, G16, IO = al("fa", NV), al("fa", 1), al("fa", L // 8)
+    ts(j5, i5, 15, None, AND)
+    KP, B1, G16, IO = al("fa", NV), al("fa", NV), al("fa", 1), al("fa", L // 8)
     cp(KP, j5)
+    ts(B1, j5, -8192.0, 4096.0, OP.mult, OP.add)
     ts(IO, i6, sl(KP, 0, 1), None, OP.add)
     ts(G16, sl(i5, 0, 1), sl(KP, 0, 1), -16.0, OP.subtract, OP.add)
-    SEL, DG, C14 = al("ba", 144), al("ba", 144), al("ba", 144)
+    SEL, DG, C14, t144 = al("ba", 144), al("ba", 144), al("ba", 144), al("ba", 144)
     ts(C14, i4, G16, None, OP.subtract)
-    ts(SEL, C14, 1.0, -BIG, OP.is_equal, OP.mult)
-    t144 = al("ba", 144)
-    ts(t144, C14, 0.0, float(2 * L), OP.is_ge, OP.mult)
-    ts(DG, C14, 1.0, None, OP.is_le)
-    tt(DG, DG, t144, OP.mult)
+    ts(SEL, C14, 1.0, -K, OP.is_equal, OP.mult)
+    ts(t144, C14, 0.5, None, OP.subtract)
+    act(t144, t144, AF.Abs)
+    ts(DG, t144, 1.0, float(2 * L), OP.is_lt, OP.mult)
 
     def mat(arena, d, w):
         m = al(arena, 128)
@@ -173,275 +190,268 @@ def build():
         act(m, src, AF.Identity, 0.0, float(w))
         return m
 
-    If, R5, R1 = mat("fa", 0, 1), mat("fa", 5, 1), mat("fa", 15, 1)
-    I32, I1184, nI = scaled("fa", If, 32), scaled("fa", If, 1184), scaled("fa", If, -1)
-    ONE = scaled("fa", ONEb, 1)
-    I8k = scaled("ba", If, 8192)
-    R5a, R5b, I25 = scaled("fa", R5, 32), scaled("fa", R5, 1184), scaled("ba", If, BIG)
-    ONE2k, nI32, Ihb, R1a = scaled("ba", ONEb, 2048), scaled("fa", If, -32), scaled("ba", If, 0.5), scaled("fa", R1, 32)
-    nONE128, Ib, nR1, nR5 = scaled("ba", ONEb, -128), scaled("ba", If, 1), scaled("fa", R1, -1), scaled("fa", R5, -1)
-    R11, R11u, R4, R10 = mat("ba", 11, 8192), mat("ba", 11, 1), mat("fa", 4, 1), mat("fa", 10, 1)
-    BK1 = scaled("ba", R11, -1)
-    BK0, BLK, b5, b0 = al("ba", 128), al("ba", 128), mat("ba", 5, 2 ** 38), mat("ba", 0, 2 ** 38)
-    tt(BK0, I8k, R11, OP.subtract)
-    tt(BLK, b5, b0, OP.subtract)
-    ts(j3, i3, 15, None, OP.bitwise_and)
-    tt(DM5, j3, tmpb, OP.add)
-    W, WR = [], []
+    I, R5, R1, R4, R11 = mat("ba", 0, 1), mat("ba", 5, 1), mat("ba", 15, 1), mat("ba", 4, 1), mat("ba", 11, 4096)
+    Ia, Ib, nI, Ih = mat("ba", 0, 2080), mat("ba", 0, 3232), mat("ba", 0, -1), mat("ba", 0, 0.5)
+    R5a, R5b, nR5, R1a = scaled("ba", R5, 2080), scaled("ba", R5, 3232), scaled("ba", R5, -1), scaled("ba", R1, 2080)
+    IK, nIK, I32, nONEK = scaled("ba", I, K), scaled("ba", I, -K), scaled("ba", I, 32), scaled("ba", ONE, -K)
+    ONE2k, nONE2k, ONE128 = scaled("ba", ONE, 2048), scaled("ba", ONE, -2048), scaled("ba", ONE, 128)
+    ONEf, R5f, R1f = scaled("fa", ONE, 1), scaled("fa", R5, 1), scaled("fa", R1, 1)
+    nR1w, nR5w, R10 = scaled("ba", R1, -8192), scaled("ba", R5, -8192), mat("ba", 10, 1)
+    diag = [[-1, 128]]
+    BK, BLK, LESS5 = mat("ba", 11, 4096), mat("ba", 5, -K * 2 ** 13), mat("ba", 5, -1)
+    select(BK, BK, diag, OP.not_equal, -4096.0, 0, 1)
+    select(BLK, BLK, diag, OP.not_equal, K * 2 ** 14, 0, 1)
+    select(LESS5, LESS5, diag, OP.not_equal, 1.0, 0, 1)
+    W = []
     for t in range(NV):
-        for lst, d, diag in ((W, DM, I8k), (WR, DM5, R11)):
-            m = al("ba", 128)
-            ts(m, d, sl(KP, t, t + 1), -8192.0, OP.is_gt, OP.mult)
-            tt(m, m, diag, OP.add)
-            lst.append(m)
-    ONES = al("ba", 2 * L)
+        m = al("ba", 128)
+        ts(m, DM, sl(KP, t, t + 1), -8192.0, OP.is_gt, OP.mult)
+        select(m, m, diag, OP.not_equal, 8192.0, 0, 1)
+        W.append(m)
+    ONES, EVEN, THIRD = al("ba", 2 * L), al("ba", 4 * L), al("ba", 3 * L)
     ms(ONES, 1.0)
+    ms(rows(EVEN, 1), 0.0)
+    ms(rows(sl(EVEN, 0, 4 * L, 2), 1), 1.0)
+    ms(rows(THIRD, 3), 0.0)
+    ms(rows(sl(THIRD, 2, 3 * L, 3), 3), 1.0)
+    ms(rows(sl(THIRD, 2, 3 * L, 3), 1), 0.0)
+    ms(rows(sl(THIRD, 0, 3 * L, 3), 1), 1.0)
     cb = {}
-    for c in (-51 * 2 ** 17, -2048, 32, -2 ** 23, 65536, -0.25, -1, -4096, 0):
-        cb[c] = al("ba", 128)
-        ms(cb[c], float(c))
 
-    def bias(out, c):
-        return (out, row(cb[c]), row(sl(ONES, 0, count(out))))
+    def bias(out, cs, pattern=None):
+        if cs not in cb:
+            cb[cs] = al("ba", 128)
+            keep = list(now)
+            now[0], now[1] = 0, -1
+            for k in range(len(cs), 0, -1):
+                ms(rows(cb[cs], k), float(cs[k - 1]))
+            now[0], now[1] = keep
+        return (out, rows(cb[cs], len(cs)), rows(pattern or sl(ONES, 0, count(out)), len(cs)))
 
-    RS = al("ba", 16 * PL)
+    ms(sl(XW0, 0, 16), 0.0)
+    RS = al("ba", 8 * L)
     ms(RS, 1.0)
-    ms(sl(RS, 0, 16 * PL, 16), 0.0)
-    ms(sl(XW, 0, XOFF), 0.0)
+    ms(sl(RS, 0, 8 * L, 16), 0.0)
 
     ps = [("ps%d" % b, 0, 512, 1, 128) for b in range(8)]
-    TH = al("fa", 16 * NV)
-    H = [al("fa", 128) for t in range(NV)]
-    HN = [al("fa", 128) for t in range(NV)]
-    ts(sl(TH, 0, 1), TI, -0.5, BIG, OP.add, OP.mult)
-    cp(H[0], HI)
 
-    def turn(t):
-        pH, pT = sl(ps[0], 384, 512), sl(ps[3], 384, 385)
-        mm([(pH, R1, H[t])])
-        act(HN[t], pH, AF.Identity)
-        send([("f", HN[t], H[t + 1])], 3.0)
-        mm([(pT, R1, sl(TH, 16 * t, 16 * t + 1))])
-        act(sl(TH, 16 * t + 16, 16 * t + 17), pT, AF.Identity)
+    def region(c, name):
+        b, k, n = (cfg["banks"][name] + (1,))[:3]
+        return sl(ps[NB * c + b], k * L, (k + n) * L)
 
-    AND, SHR = OP.bitwise_and, OP.arith_shift_right
+    TH, TB = al("fa", 16 * NV), [al("ha", L) for t in range(NV)]
+    ts(sl(TH, 0, 1), TI, -2048.0, None, OP.add)
+    for t in range(NV):
+        act(TB[t], sl(ONES, 0, L), AF.Identity, sl(TH, 16 * t, 16 * t + 1), 0.0)
+        if t < NV - 1:
+            pT = sl(ps[7], 7 * L, 7 * L + 1)
+            mm([(pT, R1f, sl(TH, 16 * t, 16 * t + 1))])
+            act(sl(TH, 16 * t + 16, 16 * t + 17), pT, AF.Identity)
+
     ch = []
     for c in range(NCH):
         now[0] = c
-        d = {"Q": al("fa", XOFF + 8 * L)}
-        for n in ("lf", "sf"):
-            d[n] = [al("fa", 3 * L) for t in range(NV + 1)]
+        d = {"Q": al("fa", 8 * L), "QO": al("fa", 8 * L), "E3": al("fa", 3 * L), "S3": al("fa", 3 * L),
+             "E4": al("ba", 4 * L), "RF1": al("ha", 4 * L), "RF": al("ha", 2 * L)}
+        for n in ("lt", "st"):
+            d[n] = [al("ha", 4 * L) for t in range(NV + 1)]
         for n in ("lb", "sb"):
-            d[n] = [al("fa", 3 * L) for t in range(NV)]
+            d[n] = [al("fa", 4 * L) for t in range(NV)]
         for n in ("lu", "su"):
             d[n] = [al("ua", L + L // 8) for t in range(NV + 1)]
-        for n in ("RF", "RF1", "d", "eq", "e", "nb", "tmp"):
+        for n in ("d", "eq", "e", "tmp"):
             d[n] = al("fa", 2 * L)
-        for n in ("t", "thA", "N0m", "J", "s", "us", "um0", "um1", "dm", "tt0", "tt1", "t2"):
+        for n in ("t0", "t1", "J", "N0m", "x", "dm", "t2", "go", "zo"):
             d[n] = al("fa", L)
         for n in ("N0", "N1", "I0", "I1", "Ng", "G", "Nx"):
             d[n] = al("ia", L)
         d["w"], d["Ix"] = al("ia", L // 8), al("ia", L + L // 8)
-        for n in ("X", "D", "AB", "Y", "SC"):
+        for n in ("X", "D", "AB", "SC"):
             d[n] = al("ba", 16 * L)
-        for n in ("nm0", "uk", "zb", "zr"):
-            d[n] = al("ba", L)
-        for n in ("u0", "u1", "um16"):
+        d["m0"], d["r"], d["Fs"] = al("ba", L), al("ha", L), al("ha", L)
+        for n in ("u0", "u1"):
             d[n] = al("ua", L)
         ch.append(d)
+        for n in d:
+            for v in (d[n] if isinstance(d[n], list) else [d[n]]):
+                named.setdefault(v[0], []).append((v[1], v[2], n))
         for b in range(4):
-            cp(sl(d["Q"], XOFF + 2 * L * b, XOFF + 2 * L * (b + 1)), sl(QI, 256 * b + 2 * L * c, 256 * b + 2 * L * (c + 1)))
-        ms(sl(d["Q"], 0, XOFF), 0.0)
-        for t in range(1, NV - 1):
-            if FUSE:
-                ms(sl(d["sb"][t], 2 * L, 3 * L), 0.0)
+            ts(sl(d["Q"], 2 * L * b, 2 * L * (b + 1)), sl(QI, 256 * b + 2 * L * c, 256 * b + 2 * L * (c + 1)),
+               2048.0, None, OP.add)
+        ms(sl(d["E3"], 0, 3 * L, 3), 0.0)
+        ms(sl(d["E4"], 0, 4 * L, 2), 0.0)
 
-    def xindex(c, Hs, Gc):
+    def xindex(c, Hc, r, ra, Gc):
         d = ch[c]
-        pp, pk = sl(ps[4 * c + 1], 6 * L, 7 * L), sl(ps[4 * c + 1], 7 * L, 8 * L)
-        act(pp, sl(Hs, L * c, L * c + L), AF.Identity, 1184.0)
-        act(pk, sl(Hs, L * c, L * c + L), AF.Identity, -4259840.0, 2080.0)
+        pp, pk = region(c, "pp"), region(c, "pk")
+        mm([bias(pp, (3232,)), (pp, r, Hc)])
+        mm([(pk, ra, Hc)])
         tt(d["t2"], pp, Gc, OP.mult)
         tt(d["Nx"], pk, d["t2"], OP.add)
         ts(sl(d["Ix"], 0, L), d["Nx"], 5, 4095, SHR, AND)
 
-    def callee(c, U):
+    def callee(c, Z):
         d = ch[c]
-        pc = sl(ps[4 * c + 2], 7 * L, 7 * L + L // 8)
-        mm([(pc, sl(DG, 14 - 2 * k, 142 - 2 * k), sl(d["zb"], k, L, 8)) for k in range(8)])
+        pc = sl(region(c, "pc"), 0, L // 8)
+        mm([(pc, sl(DG, 14 - 2 * k, 142 - 2 * k), sl(Z, k, L, 8)) for k in range(8)])
         tt(d["w"], pc, IO, OP.add)
         ts(sl(d["Ix"], L, L + L // 8), d["w"], 8 * L - 1, None, AND)
-        ts(U, d["Ix"], float(XOFF), None, OP.add)
 
-    def update(c, t):
+    def update(c, t, Q):
         d = ch[c]
-        B, win = sl(d["lb"][t], 0, 2 * L), ("ind", d["Q"], sl(d["lu"][t - 1], L, L + L // 8))
-        act(d["nb"], B, AF.Identity, 0.0, -1.0)
-        tt(d["tmp"], win, d["nb"], OP.min)
-        tt(win, d["tmp"], B, OP.max)
+        win = ("ind", Q, sl(d["lu"][t - 1], L, L + L // 8))
+        tt(d["tmp"], win, sl(d["lb"][t], 2 * L, 4 * L), OP.subtract)
+        tt(win, d["tmp"], sl(d["lb"][t], 0, 2 * L), OP.max)
 
-    def distance(c, U, pe):
+    def distance(c, pe, U, pieces, plain, terms):
         d = ch[c]
-        for k in range(NP):
-            a, b = 16 * PL * k, 16 * PL * (k + 1)
-            tt(sl(d["D"], a, b), ("ind", XW, sl(U, PL * k, PL * (k + 1))), sl(d["X"], a, b), OP.subtract)
-            act(sl(d["AB"], a, b), sl(d["D"], a, b), AF.Abs)
-        mm([(pe, sl(SEL, 15 - p, 143 - p), sl(d["AB"], p, 16 * L, 16)) for p in range(16)], "e")
-
-    def rename(c, RF, pf, sign, po, pd, halves):
-        d = ch[c]
-        e1, e2 = sl(d["e"], 0, L), sl(d["e"], L, 2 * L)
-        mm([bias(po, -1)], "s")
-        mm([bias(pd, -4096)], "s")
-        act(e1, sl(pf, 0, L), AF.Relu, -8191.0, sign)
-        act(e2, sl(pf, L, 2 * L), AF.Relu, -4096.0, sign)
-        mm([(po, ONE, e1)], "e")
-        mm([(pd, ONE, e2)], "e")
-        for h in halves:
-            tt(sl(d["eq"], h, 2 * L, 2), sl(RF, h, 2 * L, 2), po, OP.is_equal)
-        for h in halves:
-            tt(sl(d["d"], h, 2 * L, 2), sl(d["eq"], h, 2 * L, 2), pd, OP.mult)
+        for k, (a, b) in enumerate(cuts(pieces)):
+            D, X = sl(d["D"], 16 * a, 16 * b), sl(d["X"], 16 * a, 16 * b)
+            if k in plain:
+                i = act(D, ("ind", XW, sl(U, a, b)), AF.Identity)
+                diff = sl(region(c, "p4"), 0, 16 * (b - a))
+                mm([(diff, I, D), (diff, nI, X)])
+                D = diff
+            else:
+                i = tt(D, ("ind", XW, sl(U, a, b)), X, OP.subtract)
+            if k == 0:
+                mm([bias(pe, (2048 * K, 15.5 * K))] + [(pe, w, x) for w, x in terms], "s", [i])
+            act(sl(d["AB"], 16 * a, 16 * b), D, AF.Abs)
+        return mm([(pe, sl(SEL, 15 - p, 143 - p), sl(d["AB"], p, 16 * L, 16)) for p in range(16)], "e")
 
     for c in range(NCH):
         now[0] = c
         d = ch[c]
-        f0 = d["lf"][0]
+        f0 = d["lt"][0]
         ts(sl(f0, 0, L), sl(GI, L * c, L * c + L), -2048.0, None, OP.add)
-        cp(d["zb"], sl(ZI, L * c, L * c + L))
-        xindex(c, H[0], sl(f0, 0, L))
-        callee(c, d["lu"][0])
-        cp(sl(f0, L, 2 * L), sl(ZI, L * c, L * c + L))
-        ms(sl(f0, 2 * L, 3 * L), 0.0)
+        ts(sl(f0, L, 2 * L), sl(ZI, L * c, L * c + L), ZOFF, None, OP.add)
+        ts(sl(f0, 2 * L, 3 * L), sl(ZI, L * c, L * c + L), 0.0, None, OP.is_ge)
+        ts(sl(f0, 3 * L, 4 * L), sl(HI, L * c, L * c + L), -2048.0, None, OP.add)
+        xindex(c, sl(f0, 3 * L, 4 * L), I, Ia, sl(f0, 0, L))
+        callee(c, sl(f0, L, 2 * L))
+        cp(d["lu"][0], d["Ix"])
 
     def visit(c, t):
         d = ch[c]
-        pA, pB, pC, pD = ps[4 * c:4 * c + 4]
-        e0, e1, pu, pw, pF, pN = [sl(pA, k * L, k * L + L) for k in range(6)]
-        pf0, pf1, pN0, pg = sl(pB, 0, 2 * L), sl(pB, 2 * L, 4 * L), sl(pB, 4 * L, 5 * L), sl(pB, 5 * L, 6 * L)
-        po0, po1, pm1, pzz, pcnt, pm = [sl(pC, k * L, k * L + L) for k in range(6)]
-        pd0, pd1, pb, pr = sl(pD, 0, L), sl(pD, L, 2 * L), sl(pD, 2 * L, 4 * L), sl(pD, 4 * L, 6 * L)
-        zr = d["zr"]
-        dR, dF = sl(d["d"], 0, 2 * L, 2), sl(d["d"], 1, 2 * L, 2)
-        U, LF, SF, SU = d["lu"][t], d["lf"][t], d["sf"][t + 1], d["su"][t + 1]
-        Gc, Z, A = sl(LF, 0, L), sl(LF, L, 2 * L), sl(LF, 2 * L, 3 * L)
-        Hc = sl(H[t], L * c, L * c + L)
-        RF, RF1, nm0, uk = d["RF"], d["RF1"], d["nm0"], d["uk"]
-        R, F, Ra, Fa = sl(RF, 0, 2 * L, 2), sl(RF, 1, 2 * L, 2), sl(RF1, 0, 2 * L, 2), sl(RF1, 1, 2 * L, 2)
+        pN0, pN, pe, pf, po, p4, p3, pF, pw, pwk, pzr, pz, pM, pb = [
+            region(c, n) for n in "pN0 pN e0 pf0 po0 p4 p3 pF pw pwk pzr pz pM pb".split()]
+        fa, fb = sl(pf, 0, L), sl(pf, L, 2 * L)
+        U, LT, ST, SU = d["lu"][t], d["lt"][t], d["st"][t + 1], d["su"][t + 1]
+        Gc, Z, UP, Hc = [sl(LT, k * L, k * L + L) for k in range(4)]
+        Gn, Zn, un1, Hn = [sl(ST, k * L, k * L + L) for k in range(4)]
+        RF, m0, e1, e2 = d["RF"], d["m0"], sl(d["e"], 0, L), sl(d["e"], L, 2 * L)
+        R, F = sl(RF, 0, 2 * L, 2), sl(RF, 1, 2 * L, 2)
+        RF1, Ra, Fa = sl(d["RF1"], 1, 4 * L, 2), sl(d["RF1"], 1, 4 * L, 4), sl(d["RF1"], 3, 4 * L, 4)
         last = t == NV - 1
+        before = [(IK, TB[t]), (nONEK, UP)]
         if t > 1:
-            update(c, t - 1)
-        act(RF, ("ind", d["Q"], sl(U, L, L + L // 8)), AF.Identity)
-        for k in range(NP):
-            act(sl(d["X"], 16 * PL * k, 16 * PL * (k + 1)), ("ind", XW, sl(U, PL * k, PL * (k + 1))), AF.Identity)
-        mm([bias(pN0, -51 * 2 ** 17)], "s")
-        mm([(pN0, I32, R), (pN0, I1184, F)], "e")
-        tt(d["t"], R, F, OP.mult)
-        tt(d["N0"], d["t"], pN0, OP.add)
+            update(c, t - 1, d["Q"])
+        act(RF, ("ind", d["Q"], sl(U, L, L + L // 8)), AF.Identity, -4096.0)
+        for k, (a, b) in enumerate(cuts(cfg["xp"])):
+            if k in cfg["xonv"][c]:
+                cp(sl(d["X"], 16 * a, 16 * b), ("ind", XW, sl(U, a, b)))
+            else:
+                act(sl(d["X"], 16 * a, 16 * b), ("ind", XW, sl(U, a, b)), AF.Identity)
+        if last:
+            act(d["QO"], d["Q"], AF.Identity, -2048.0)
+        mm([(pN0, Ia, R), (pN0, Ib, F)])
+        tt(d["t0"], R, F, OP.mult)
+        tt(d["N0"], d["t0"], pN0, OP.add)
         ts(d["I0"], d["N0"], 5, 4095, SHR, AND)
-        ts(d["u0"], d["I0"], float(XOFF), None, OP.add)
-        act(d["thA"], A, AF.Identity, sl(TH, 16 * t, 16 * t + 1), BIG)
-        act(zr, Z, AF.Identity)
-        mm([bias(pu, 32), (pu, ONEb, zr)])
-        mm([bias(pw, -2 ** 23), (pw, ONE2k, zr), (pw, nI32, Gc)])
-        act(d["us"], pu, AF.Identity)
-        mm([(e0, If, d["thA"])], "s")
-        fa, fb = sl(pf0, 0, L), sl(pf0, L, 2 * L)
-        mm([bias(pf0, 0)], "s")
-        mm([(fa, nI, R)], "")
-        mm([(fb, nI, Hc)], "")
-        mm([(fb, If, R)], "")
-        if PRP:
-            mm([(pr, If, RF)])
-        distance(c, d["u0"], e0)
-        ts(nm0, e0, 0.0, -1.0, OP.is_gt, OP.mult)
-        mm([(fa, W[t], nm0), (fb, W[t], nm0)], "e")
-        mm([bias(pN, -51 * 2 ** 17), (pN, I25, nm0)], "s")
-        if N1D:
-            mm([(pN, R5a, R)], "")
-            mm([(pN, R5b, F)], "")
-        tt(d["N0m"], d["N0"], e0, OP.min)
-        tt(d["um0"], pu, nm0, OP.mult)
-        rename(c, RF, pf0, -1.0, po0, pd0, (0, 1))
-        tt(RF1, pr if PRP else RF, d["d"], OP.add)
-        tt(d["t"], Ra, Fa, OP.mult)
-        mm([(pN, R5a, dR if N1D else Ra)], "")
-        mm([(pN, R5b, dF if N1D else Fa)], "")
-        mm([(pN, R5, d["t"])], "e")
+        cp(d["u0"], d["I0"])
+        sums = distance(c, pe, d["u0"], cfg["p0"], cfg["plain0"][c], before)
+        mm([bias(pf, (0,)), (fa, I, R), (fb, I, Hc), (fb, nI, R)], "s", [sums])
+        mark = act(m0, pe, AF.Sigmoid, 0.0, 2.0 ** -16)
+        mm([(fa, W[t], m0), (fb, W[t], m0)], "e")
+        tt(d["N0m"], d["N0"], pe, OP.min)
+        mm([bias(po, (-4096,))], "s", [mark])
+        mm([bias(p4, (-4096,), EVEN), (sl(p4, 1, 4 * L, 2), I, RF)], "s", [sums])
+        act(d["e"], pf, AF.Relu, -4096.0)
+        mm([(po, ONEf, e1)], "e")
+        mm([(sl(p4, 0, 4 * L, 4), ONEf, e2), (sl(p4, 2, 4 * L, 4), ONEf, e2)], "e")
+        tt(sl(d["E4"], 1, 4 * L, 4), R, po, OP.is_equal)
+        tt(sl(d["E4"], 3, 4 * L, 4), F, po, OP.is_equal)
+        scan(d["RF1"], d["E4"], p4, OP.add)
+        tt(d["t1"], Ra, Fa, OP.mult)
+        mm([(pN, R5a, Ra), (pN, R5b, Fa), (pN, nIK, m0)], "s")
+        mm([(pN, R5f, d["t1"])], "e")
         tt(d["N1"], pN, d["N0m"], OP.max)
         ts(d["I1"], d["N1"], 5, 4095, SHR, AND)
-        ts(d["u1"], d["I1"], float(XOFF), None, OP.add)
-        ra, rb, rc, rd = (R5, R5a, nR5, R10) if last else (R1, R1a, nR1, R4)
-        fa, fb = sl(pf1, 0, L), sl(pf1, L, 2 * L)
-        mm([(e1, If, d["thA"]), (e1, BLK, nm0)], "s")
-        mm([bias(pf1, 0), (fb, If, Hc)], "s")
-        mm([(fa, If, Ra), (fa, WR[t], nm0)], "")
-        mm([(fb, nR5, Ra), (fb, W[t], nm0)], "")
-        mm([(pm1, R11u, nm0)], "s")
-        if t > 0:
-            mm([(pb, If, RF1)], "s")
-            mm([(sl(pb, h, 2 * L, 2), BK0, nm0) for h in range(2)], "")
-        distance(c, d["u1"], e1)
-        ts(uk, e1, 0.0, None, OP.is_gt)
-        mm([(fa, WR[t], uk), (fb, W[t], uk)], "e")
-        tt(d["J"], d["I1"], e1, OP.min)
-        ts(d["um16"], d["J"], float(-XOFF), float(XOFF), OP.max, OP.add)
-        mm([(pm1, R11u, uk)], "e")
-        if t > 0:
-            mm([(sl(pb, h, 2 * L, 2), BK1, uk) for h in range(2)], "e")
-        mm([bias(pF, -2048), (pF, If, Fa)], "s")
-        mm([bias(pg, 65536), (pg, rb, Gc)], "s")
-        tt(d["um1"], pm1, d["us"], OP.mult)
-        tt(d["dm"], pw, uk, OP.mult)
-        mm([(pg, ra, d["dm"])], "")
-        rename(c, RF1, pf1, 1.0, po1, pd1, (1, 0) if t > 0 else (1,))
-        mm([(pzz, Ib, zr), (pzz, nONE128, uk)])
-        if not last:
-            mm([(pcnt, ONEb, uk)])
-            act(sl(SF, 2 * L, 3 * L), pcnt, AF.Identity)
-        mm([(pF, If, dF)], "e")
-        tt(d["tt0"], pF, d["um0"], OP.mult)
-        tt(d["tt1"], pF, d["um1"], OP.mult)
-        mm([(pg, rc, d["tt0"])], "")
-        mm([(pg, rd, d["tt1"])], "e")
-        cp(d["Ng"], pg)
+        cp(d["u1"], d["I1"])
+        raf, rd, nrw = (R5f, R10, nR5w) if last else (R1f, R4, nR1w)
+        mm([(pF, LESS5, Fa)])
+        tt(d["x"], pF, m0, OP.mult)
+        mm([(pF, rd, Fa), (pF, raf, d["x"])])
+        act(d["Fs"], pF, AF.Identity)
+        pe, pf, po = region(c, "e1"), region(c, "pf1"), region(c, "po1")
+        fa, fb = sl(pf, 0, L), sl(pf, L, 2 * L)
+        sums = distance(c, pe, d["u1"], cfg["p1"], cfg["plain1"][c], before + [(BLK, m0)])
+        mm([bias(pf, (0,)), (fa, nR5, Ra), (fa, W[t], m0), (fb, nI, Hc), (fb, R5, Ra), (fb, W[t], m0)], "s", [sums])
+        mark = act(un1, pe, AF.Sigmoid, 0.0, -2.0 ** -16)
+        mm([(fa, W[t], un1), (fb, W[t], un1)], "e")
+        mm([bias(po, (-4096,))], "s", [mark])
+        mm([bias(p3, (-4096, -896 * 2 ** 16, 2 ** 16), THIRD), (sl(p3, 1, 3 * L, 3), I, d["Fs"]),
+            (sl(p3, 2, 3 * L, 3), ONE2k, Z)], "s", [sums])
+        act(d["e"], pf, AF.Relu, sl(B1, t, t + 1), -1.0)
+        mm([(po, ONEf, e1)], "e")
+        tt(d["J"], d["I1"], pe, OP.min)
+        ts(d["u0"], d["J"], 16.0, 0.0, OP.add, OP.max)
+        for k, (a, b) in enumerate(cuts(cfg["ps"])):
+            Y, src = sl(d["AB"], 16 * a, 16 * b), ("ind", XW0, sl(d["u0"], a, b))
+            if k in cfg["onv"][c]:
+                ts(Y, src, 0.5, None, OP.mult)
+            else:
+                act(Y, src, AF.Identity, 0.0, 0.5)
+            scan(sl(d["SC"], 16 * a, 16 * b), sl(RS, 0, 16 * (b - a)), Y, OP.max)
+        mm([(pzr, Ih, Z), (pzr, ONE128, un1)])
+        act(d["r"], pzr, AF.Relu, 0.25 - ZOFF / 2 - 2048.0)
+        mm([bias(pz, (ZOFF / 2, -0.25)), (pz, Ih, Z), (pz, I, d["r"])])
+        tt(Zn, sl(d["SC"], 15, 16 * L, 16), pz, OP.add)
+        mm([(pwk, ONE, Z), (pwk, nrw, un1)])
+        act(sl(d["E3"], 2, 3 * L, 3), pwk, AF.Relu, 32.0 - 16 * ZOFF)
+        mm([bias(pw, (3 * 2 ** 24,)), (pw, nONE2k, Z), (pw, I32, Gc)])
+        tt(d["dm"], pw, un1, OP.mult)
+        mm([(sl(p3, 2, 3 * L, 3), raf, d["dm"])], "")
+        mm([(sl(p3, 0, 3 * L, 3), ONEf, e2)], "e")
+        tt(sl(d["E3"], 1, 3 * L, 3), d["Fs"], po, OP.is_equal)
+        scan(d["S3"], d["E3"], p3, OP.add)
+        cp(d["Ng"], sl(d["S3"], 2, 3 * L, 3))
         ts(d["G"], d["Ng"], 5, 4095, SHR, AND)
-        ts(sl(SF, 0, L), d["G"], 0.0 if last else -2048.0, None, OP.add)
-        if not last:
-            xindex(c, HN[t], sl(SF, 0, L))
         if t > 0:
+            for h in range(2):
+                mm([(sl(pM, h, 2 * L, 2), R11, un1), (sl(pM, h, 2 * L, 2), BK, m0)])
+            act(sl(d["sb"][t], 2 * L, 4 * L), pM, AF.Identity)
+            mm(([bias(pb, (-2048,))] if last else []) + [(pb, I, RF1)] +
+               [(sl(pb, h, 2 * L, 2), w, x) for h in range(2) for w, x in ((R11, un1), (BK, m0))])
+            for h, x in enumerate((Ra, Fa)):
+                tt(sl(d["eq"], h, 2 * L, 2), x, po, OP.is_equal)
+            for h in range(2):
+                tt(sl(d["d"], h, 2 * L, 2), sl(d["eq"], h, 2 * L, 2), sl(p3, 0, 3 * L, 3), OP.mult)
             tt(sl(d["sb"][t], 0, 2 * L), pb, d["d"], OP.add)
-        for k in range(NP):
-            a, b = 16 * PL * k, 16 * PL * (k + 1)
-            act(sl(d["Y"], a, b), ("ind", XW, sl(d["um16"], PL * k, PL * (k + 1))), AF.Identity)
-            scan(sl(d["SC"], a, b), RS, sl(d["Y"], a, b))
-        mm([bias(pm, -0.25), (pm, Ihb, zr), (pm, Ihb, sl(d["SC"], 15, 16 * L, 16))])
-        ts(d["s"], pm, MAGIC, -MAGIC, OP.add, OP.add)
-        tt(d["zb"], d["s"], pzz, OP.max)
-        act(sl(SF, L, 2 * L), d["zb"], AF.Identity)
-        back = ("b", sl(d["sb"][t], 0, 2 * L), sl(d["lb"][t], 0, 2 * L))
+            send("b", d["sb"][t], d["lb"][t], 2.7)
         if last:
-            send([back], 2.5)
-            dma("Y", ("hbm", "yg", L * c, L * c + L), sl(SF, 0, L), 2.0)
-            dma("Y", ("hbm", "yz", L * c, L * c + L), sl(SF, L, 2 * L), 2.0)
-            update(c, t)
+            cp(d["go"], d["G"])
+            act(d["zo"], Zn, AF.Identity, -ZOFF)
+            dma("Y", ("hbm", "yg", L * c, L * c + L), d["go"], 2.0)
+            dma("Y", ("hbm", "yz", L * c, L * c + L), d["zo"], 2.0)
+            update(c, t, d["QO"])
             for b in range(4):
                 dma("YS"[b % 2], ("hbm", "yq", 256 * b + 2 * L * c, 256 * b + 2 * L * (c + 1)),
-                    sl(d["Q"], XOFF + 2 * L * b, XOFF + 2 * L * (b + 1)), 2.2)
+                    sl(d["QO"], 2 * L * b, 2 * L * (b + 1)), 2.2)
         else:
-            callee(c, SU)
-            if FUSE and t > 0:
-                send([("f", SF, d["lf"][t + 1]), ("b", d["sb"][t], d["lb"][t])], 2.8)
-            else:
-                if t > 0:
-                    send([back], 2.5)
-                send([("f", SF, d["lf"][t + 1])], 2.8)
-            send([("f", SU, d["lu"][t + 1])], 2.2)
+            mm([(region(c, "pH"), R1, Hc)])
+            act(Hn, region(c, "pH"), AF.Identity)
+            ts(Gn, d["G"], -2048.0, None, OP.add)
+            xindex(c, Hc, R1, R1a, Gn)
+            callee(c, Zn)
+            lists = []
+            for a, b in (((L, L + L // 8), (0, L)) if cfg["split"] else ((0, L + L // 8),)):
+                cp(sl(SU, a, b), sl(d["Ix"], a, b))
+                lists.append(send("f", sl(SU, a, b), sl(d["lu"][t + 1], a, b), 2.2))
+            send("f", ST, d["lt"][t + 1], 2.4, lists)
 
     for t in range(NV):
         now[1] = t
-        if t < NV - 1:
-            now[0] = 0
-            turn(t)
         for c in range(NCH):
             now[0] = c
             visit(c, t)
@@ -451,17 +461,14 @@ def build():
 def depend(ops):
     hist = {}
     for i, o in enumerate(ops):
-        hard, soft = set(), set()
-        for j in o["extra"]:
-            (hard if o["eng"] == "R" else soft).add(j)
+        hard, soft = set(), set(o["extra"])
+        if o["eng"] == "R":
+            hard, soft = soft, hard
         for kind, sp in (("r", o["r"]), ("w", o["w"])):
             for name, a, b, st in sp:
                 for j, k2, a2, b2, st2 in hist.get(name, []):
-                    if j != i and a < b2 and a2 < b and (kind == "w" or k2 == "w") and (st != st2 or (a - a2) % st == 0):
-                        if ops[j]["eng"] == "P" and o["eng"] == "P":
-                            soft.add(j)
-                        else:
-                            hard.add(j)
+                    if j != i and a < b2 and a2 < b and (kind == "w" or k2 == "w") and (a - a2) % math.gcd(st, st2) == 0:
+                        (soft if ops[j]["eng"] == "P" and o["eng"] == "P" else hard).add(j)
         for name, a, b, st in o["w"]:
             hist[name] = [h for h in hist.get(name, [])
                           if not (a <= h[2] and h[3] <= b and (st == 1 or (st == h[4] and (a - h[2]) % st == 0)))]
@@ -471,34 +478,41 @@ def depend(ops):
         o["data"], o["soft"] = hard, soft - hard
 
 
-def schedule(ops, lead, look, step, shift):
+def label(o):
+    if o["slot"] is None:
+        return None
+    e, name, a, k = o["slot"]
+    if name.startswith("ps"):
+        name = "bank%d" % (int(name[2]) % NB)
+    return "%s %s %d %d" % (e, name, a, k)
+
+
+def schedule(ops, lead, look, shift):
     n = len(ops)
-    for o in ops:
-        o["hard"] = set(o["data"])
-    succ = [[] for i in range(n)]
-    left = [0] * n
+    succ, left = [[] for i in range(n)], [0] * n
     for i, o in enumerate(ops):
-        for j in o["hard"] | o["soft"]:
+        for j in o["data"] | o["soft"]:
             succ[j].append(i)
             left[i] += 1
-    prio = [0.0] * n
+    prio, bulk = [0.0] * n, {}
     for i in range(n - 1, -1, -1):
         o = ops[i]
         best = o["lat"]
         for s in succ[i]:
-            best = max(best, prio[s] + (o["lat"] + HOP if i in ops[s]["hard"] else 0.0))
+            best = max(best, prio[s] + (o["lat"] + HOP if i in ops[s]["data"] else 0.0))
+        if o["busy"] > 0.3 and o["eng"] in "VS":
+            kind = (o["eng"], o["chunk"], o["visit"])
+            best = max(best, bulk.get(kind, 0.0))
+            bulk[kind] = best + o["busy"]
         prio[i] = best + o["busy"]
     for i in range(n):
-        k = ops[i]["slot"]
-        prio[i] += (lead if ops[i]["chunk"] == 0 else 0.0) + (step * (ord(shift[k]) - 77) if k < len(shift) else 0.0)
-    free, bank, done, order = {}, {}, [0.0] * n, []
+        prio[i] += (lead if ops[i]["chunk"] == 0 else 0.0) + shift.get(label(ops[i]), 0.0)
+    free, bank, done, held, due, taken = {}, {}, [0.0] * n, {}, [0.0] * n, []
     ready = [i for i in range(n) if left[i] == 0]
 
     def start(i):
         o = ops[i]
-        s = free.get(o["eng"], 0.0) if o["eng"] != "R" else 0.0
-        for j in o["hard"]:
-            s = max(s, done[j] + HOP)
+        s = max(due[i], free.get(o["eng"], 0.0) if o["eng"] != "R" else 0.0)
         for b in o["banks"]:
             for e, j in bank.get(b, {}).items():
                 if e != o["eng"]:
@@ -506,45 +520,214 @@ def schedule(ops, lead, look, step, shift):
         return s
 
     while ready:
-        st = [(start(i), i) for i in ready]
+        st = [(start(i), i) for i in ready
+              if ops[i]["eng"] != "P" or held.get(ops[i]["banks"][0]) in (None, ops[i]["group"])]
         s0, i0 = min(st)
         cand = [(prio[i], -i, s) for s, i in st if ops[i]["eng"] == ops[i0]["eng"] and s <= s0 + look * ops[i0]["busy"]]
         p, i, s = max(cand)
         i = -i
         o = ops[i]
         for b in o["banks"]:
-            for e, j in bank.get(b, {}).items():
-                if e != o["eng"]:
-                    o["hard"].add(j)
             bank.setdefault(b, {})[o["eng"]] = i
-        o["start"] = s
+            if o["group"] is not None:
+                held[b] = None if o["args"][2] else o["group"]
+        o["start"], o["turn"] = s, len(taken)
+        taken.append(i)
         free[o["eng"]] = s + o["busy"]
         done[i] = s + o["busy"] + o["lat"]
-        order.append(i)
         ready.remove(i)
         for k in succ[i]:
+            due[k] = max(due[k], done[i] + HOP if i in ops[k]["data"] else s)
             left[k] -= 1
             if left[k] == 0:
                 ready.append(k)
-    need = set()
-    for o in ops:
+    return max(done)
+
+
+def repeat(ops):
+    n = len(ops)
+    slot = {(o["slot"], o["chunk"]): o["start"] + 1e-7 * i for i, o in enumerate(ops) if o["visit"] == 2}
+    firsts = [min(o["start"] for o in ops if o["visit"] == t and o["kind"] == "send") for t in (2, 3)]
+    beat = firsts[1] - firsts[0]
+    key = [slot[(o["slot"], o["chunk"])] + beat * (o["visit"] - 2) if (o["slot"], o["chunk"]) in slot else None for o in ops]
+    late = [1e9] * n
+    for i in range(n - 1, -1, -1):
+        if key[i] is None and late[i] < 1e9:
+            key[i] = late[i] - ops[i]["busy"] - ops[i]["lat"] - HOP
+        for j in ops[i]["data"] | ops[i]["soft"]:
+            late[j] = min(late[j], 1e9 if key[i] is None else key[i])
+    succ, left = [[] for i in range(n)], [0] * n
+    for i, o in enumerate(ops):
+        if key[i] is None:
+            key[i] = max([key[j] + ops[j]["busy"] + ops[j]["lat"] for j in o["data"] | o["soft"]] + [0.0])
+        for j in o["data"] | o["soft"]:
+            succ[j].append(i)
+            left[i] += 1
+    ready, held, now = [i for i in range(n) if left[i] == 0], {}, -1e9
+    while ready:
+        i = min((key[i], i) for i in ready
+                if ops[i]["group"] is None or held.get(ops[i]["banks"][0]) in (None, ops[i]["group"]))[1]
+        ready.remove(i)
+        key[i] = now = max(key[i], now + 1e-7)
+        if ops[i]["group"] is not None:
+            held[ops[i]["banks"][0]] = None if ops[i]["args"][2] else ops[i]["group"]
+        for j in succ[i]:
+            left[j] -= 1
+            if left[j] == 0:
+                ready.append(j)
+    return key, beat, slot
+
+
+def improve(ops, key, beat, slot, tries, heat, seed):
+    n = len(ops)
+    names, var, shift, phase = {}, [], [], []
+    for i, o in enumerate(ops):
+        name = (o["slot"], o["chunk"]) if 0 < o["visit"] < NV - 1 and (o["slot"], o["chunk"]) in slot else i
+        shift.append(beat * max(o["visit"], 0))
+        if name not in names:
+            names[name] = len(phase)
+            phase.append(key[i] - shift[i])
+        var.append(names[name])
+    up, down, info = {}, {}, []
+    for i, o in enumerate(ops):
+        for j in sorted(o["data"] | o["soft"]):
+            if var[i] != var[j]:
+                up.setdefault(var[i], {})[(var[j], shift[i] - shift[j])] = 1
+                down.setdefault(var[j], {})[(var[i], shift[i] - shift[j])] = 1
+        pre = [(j, ops[j]["lat"] + HOP) for j in o["data"]] + [(j, 0.0) for j in o["soft"]]
+        info.append((pre, "VSPGYR".index(o["eng"]), o["busy"], [int(b[2]) for b in o["banks"]], o["lat"] + HOP, o["group"],
+                     None if o["group"] is None or o["args"][2] else o["group"]))
+    state = [seed]
+
+    def draw():
+        state[0] = (state[0] * 1103515245 + 12345) % 2 ** 31
+        return state[0] / 2 ** 31
+
+    def run(ph):
+        end, why, ready = [None] * n, [-1] * n, [0.0] * n
+        last, held, bank = [-1] * 6, [None] * 8, [[-1, -1, -1] for b in range(8)]
+        for x, i in sorted((ph[var[i]] + shift[i], i) for i in range(n)):
+            pre, e, busy, banks, tail, group, keeps = info[i]
+            s, w = 0.0, -1
+            for j, gap in pre:
+                x = end[j]
+                if x is None:
+                    return None
+                if x + gap > s:
+                    s, w = x + gap, j
+            ready[i] = s
+            if e < 5:
+                p = last[e]
+                if p >= 0 and end[p] > s:
+                    s, w = end[p], p + n
+                last[e] = i
+            for b in banks:
+                m = bank[b]
+                for e2 in (0, 1, 2):
+                    p = m[e2]
+                    if e2 != e and p >= 0 and end[p] + info[p][4] > s:
+                        s, w = end[p] + info[p][4], p + n
+                m[e] = i
+                if e == 2:
+                    if held[b] is not None and held[b] != group:
+                        return None
+                    held[b] = keeps
+            end[i], why[i] = s + busy, w
+        return max(end[i] + info[i][4] for i in range(n)) + 0.3 * sum(end) / n, end, why, ready
+
+    def waits(r):
+        end, why = r[1], r[2]
+        x = max((end[i] + info[i][4], i) for i in range(n))[1]
+        path = []
+        while why[x] >= 0:
+            if why[x] >= n and var[why[x] - n] != var[x]:
+                path.append((why[x] - n, x))
+            x = why[x] % n
+        return path, [(w - n, i) for i, w in enumerate(why) if w >= n and var[w - n] != var[i]]
+
+    def move(ph, v, to, side, sign):
+        ph[v] = to
+        for u, d in side.get(v, ()):
+            if sign * (ph[u] - (to + sign * d)) >= 0:
+                move(ph, u, to + sign * d - sign * 1e-6 * (1 + draw()), side, sign)
+
+    cur = run(phase)
+    if cur is None:
+        return key
+    path, more = waits(cur)
+    best = (cur[0], list(phase))
+    for t in range(tries):
+        pick = path if draw() < 0.8 and path else more
+        p, x = pick[int(draw() * len(pick))]
+        new, kind = list(phase), draw()
+        if kind < 0.3:
+            late = cur[3][x] + 0.3 * draw() - 0.1
+            p = min((cur[1][q], q) for q in range(n) if info[q][1] == info[x][1] and cur[1][q] - info[q][2] >= late or q == x)[1]
+            if var[p] == var[x]:
+                continue
+        d = shift[x] - shift[p]
+        if kind < 0.65:
+            move(new, var[x], phase[var[p]] - d - 1e-5 * (1 + draw()), up, 1)
+        else:
+            move(new, var[p], phase[var[x]] + d + 1e-5 * (1 + draw()), down, -1)
+        r = run(new)
+        if r is not None and r[0] <= cur[0] + heat * draw() ** 3 * (1 - t / tries):
+            phase, cur = new, r
+            path, more = waits(cur)
+            if r[0] < best[0]:
+                best = (r[0], list(phase))
+    return [best[1][var[i]] + shift[i] for i in range(n)]
+
+
+def finish(ops, key):
+    order = [i for x, i in sorted((key[i], i) for i in range(len(ops)))]
+    done, free, bank, need, cnt = {}, {}, {}, set(), {}
+    known = {}
+    for k, i in enumerate(order):
+        o = ops[i]
+        hard = set(o["data"])
+        for b in o["banks"]:
+            hard |= set(j for e, j in bank.get(b, {}).items() if e != o["eng"])
+            bank.setdefault(b, {})[o["eng"]] = i
+        o["start"] = max([free.get(o["eng"], 0.0) if o["eng"] != "R" else 0.0] + [done[j] + HOP for j in hard])
+        free[o["eng"]] = o["start"] + o["busy"]
+        done[i] = o["start"] + o["busy"] + o["lat"]
+        o["place"], o["hard"] = k, set()
+        mine = known.setdefault(o["eng"], {})
+        for x, j in sorted(((ops[j]["place"], j) for j in hard), reverse=True):
+            p = ops[j]
+            if p["sem"] is not None or o["eng"] == "R":
+                o["hard"].add(j)
+            elif mine.get(p["eng"], -1) < x:
+                o["hard"].add(j)
+                mine[p["eng"]] = x
+                for e in p["knows"]:
+                    mine[e] = max(mine.get(e, -1), p["knows"][e])
+        o["knows"] = dict(mine)
         need |= o["hard"]
-    cnt = {}
     for i in order:
         o = ops[i]
         o["inc"] = None
         if o["sem"] is None and o["kind"] != "send" and i in need:
             cnt[o["eng"]] = cnt.get(o["eng"], 0) + 1
             o["inc"] = cnt[o["eng"]]
-    return order, cnt, max(done)
+    return order, cnt, max(done.values())
 
 
-OPS, SEMS, TOP = build()
-depend(OPS)
-ORDER, TOTAL, SPAN = schedule(OPS, *PLAN)
+def plan(cfg):
+    ops, sems, top = build(cfg)
+    depend(ops)
+    schedule(ops, cfg["lead"], cfg["look"], cfg["shift"])
+    key = [o["start"] + 1e-7 * o["turn"] for o in ops]
+    key = [i - 1e6 if o["kind"] == "dma" and o["visit"] < 0 else key[i] for i, o in enumerate(ops)]
+    return (ops, sems, top) + finish(ops, key)
+
+
+OPS, SEMS, TOP, ORDER, TOTAL, SPAN = plan(CFG)
 
 SCRATCH = {"fa": ("sbuf", [128, TOP["fa"]], "float32"), "ba": ("sbuf", [128, TOP["ba"]], "bfloat16"),
-           "ia": ("sbuf", [128, TOP["ia"]], "int32"), "ua": ("sbuf", [128, TOP["ua"]], "uint16")}
+           "ha": ("sbuf", [128, TOP["ha"]], "float16"), "ia": ("sbuf", [128, TOP["ia"]], "int32"),
+           "ua": ("sbuf", [128, TOP["ua"]], "uint16")}
 for _b in range(8):
     SCRATCH["ps%d" % _b] = ("psum", [128, 512], "float32")
 SEMAPHORES = ["qV", "qS", "qP", "qG", "sent"] + SEMS
@@ -626,11 +809,13 @@ def rank_program(g, core, T, topo):
         elif k == "ms":
             ins = q.memset(ap(a[0]), a[1])
         elif k == "scan":
-            ins = q.tensor_tensor_scan(ap(a[0]), ap(a[1]), ap(a[2]), 0.0, OP.mult, OP.max)
+            ins = q.tensor_tensor_scan(ap(a[0]), ap(a[1]), ap(a[2]), 0.0, OP.mult, a[3])
         elif k == "act":
             ins = q.activation(ap(a[0]), ap(a[1]), a[2], bias=ap(a[3]), scale=ap(a[4]))
         elif k == "iota":
             ins = q.iota(ap(a[0]), a[1], a[2], a[3])
+        elif k == "sel":
+            ins = q.affine_select(ap(a[0]), ap(a[1]), a[2], a[3], a[4], a[5], a[6])
         elif k == "mm":
             for m, (x, w, y) in enumerate(a[0]):
                 ins = q.matmul(ap(x), ap(w), ap(y), a[1] and m == 0, a[2] and m == len(a[0]) - 1)
@@ -639,18 +824,10 @@ def rank_program(g, core, T, topo):
             final[o["sem"]] = 16
             continue
         else:
-            if len(a) == 1:
-                d, src, dst, s = a[0]
-                rid, pid, se = topo.addr(dest[d])
-                g.remote_dma(ap(dst), ap(src), T.sem[s], T.sem.sent, pid, rid, mask(d))
-            else:
-                trs = []
-                for d, src, dst, s in a:
-                    rid, pid, se = topo.addr(dest[d])
-                    trs.append(RemoteDMATransfer(dst_ids=[DstId(rid=rid, pnc=pid)], dma_engine_mask=mask(d),
-                                                 remote_sem=T.sem[s], src=ap(src), dst=ap(dst)))
-                g.remote_dma_fused(trs, local_sem=T.sem.sent)
-            sent[0] += sum(len(mine[it[0]]) for it in a)
+            d, src, dst, s = a[0]
+            rid, pid, se = topo.addr(dest[d])
+            g.remote_dma(ap(dst), ap(src), T.sem[s], T.sem.sent, pid, rid, mask(d))
+            sent[0] += len(mine[d])
             continue
         if o["inc"] is not None:
             ins.then_inc(T.sem["q" + e], 1)

import math
from concourse.bass import DstId, RemoteDMATransfer
from concourse.mybir import AluOpType as OP, ActivationFunctionType as AF

NCH, L, NV, NB = 2, 64, 6, 4
ZOFF = 1536.0
CY, PCY, HOP = 1.0e-3, 0.52e-3, 0.16
GCY, SCY, SEND = 1.56, 3.8, 0.8
SHIFT = {'P bank0 448 1': 5.5, 'V SC 256 1': -6.0, 'S Fs 0 1': -3.8, 'S X 0 1': -1.8, 'V su 0 1': -3.6, 'P bank1 192 1': -7.8, 'V AB 768 1': -0.7, 'S AB 0 2': -1.0, 'S sb 128 1': -3.3, 'V D 512 1': -3.7, 'V dm 0 1': -0.5, 'V SC 0 1': 5.9, 'P bank2 256 2': -3.4, 'S m0 0 1': 0.9, 'S D 768 1': 4.9, 'P bank3 64 2': 2.0, 'V sb 0 1': 2.1, 'V SC 512 1': 0.5, 'V D 0 1': 1.5, 'V tmp 0 1': 0.7, 'Y zo 0 1': 5.1, 'P bank1 128 2': 3.1, 'V eq 0 1': 2.4, 'V S3 0 1': 1.9, 'S X 512 1': -0.7, 'G st 0 1': -0.4, 'P bank0 128 1': 0.1, 'S AB 512 2': 0.4, 'S AB 256 1': -0.8, 'P bank0 192 1': -0.6, 'P bank1 448 1': -1.8, 'V d 0 1': 2.2, 'S AB 256 3': 0.1, 'S e 0 2': 1.3, 'S X 256 1': 0.4, 'V QO 0 1': -0.8, 'V tmp 0 2': -0.4, 'S st 192 1': -0.3, 'V w 0 1': 0.3, 'V eq 1 1': -0.2, 'V t0 0 1': 1.0, 'S RF 0 1': -0.3, 'V D 256 2': 0.1, 'V t1 0 1': -1.7, 'V N0m 0 1': -0.1, 'V Ng 0 1': -0.3, 'R lu 0 1': 0.6, 'S AB 256 2': 1.3, 'P bank1 128 1': -1.6, 'V st 0 1': -0.2}
CFG = {"lead": 4.1, "look": 0.3, "shift": SHIFT, "split": True,
       "xp": (16, 16, 16, 16), "p0": (16, 16, 16, 16), "p1": (16, 16, 16, 16), "ps": (16, 16, 16, 16), "onv": ((3,), (3,)),
       "xonv": ((), ()), "plain0": ((), ()), "plain1": ((3,), (3,)),
       "banks": {"pN0": (1, 0), "e0": (3, 0), "pf0": (0, 0, 2), "po0": (1, 1), "p4": (2, 0, 4), "pN": (1, 2),
                 "pF": (0, 2), "pH": (0, 3), "e1": (3, 1), "pf1": (0, 0, 2), "po1": (1, 1), "p3": (2, 4, 3),
                 "pM": (0, 4, 2), "pwk": (0, 6), "pzr": (0, 7), "pb": (1, 3, 2), "pw": (1, 5), "pz": (3, 2),
                 "pc": (3, 3), "pp": (1, 6), "pk": (1, 7)}}


def sl(v, a, b, step=1):
    return (v[0], v[1] + a, v[1] + b, step, v[4])


def rows(v, n):
    return (v[0], v[1], v[2], v[3], n)


def count(v):
    if v[0] == "ind":
        return 16 * count(v[2])
    return (v[2] - v[1] + v[3] - 1) // v[3]


def isap(v):
    return isinstance(v, tuple)


def cuts(sizes):
    out, a = [], 0
    for s in sizes:
        out.append((a, a + s))
        a += s
    return out


def build(cfg):
    top = {"fa": 0, "ba": 0, "ha": 0, "ia": 0, "ua": 0}
    ops, sems = [], []
    opened, named, seen = {}, {}, {}
    now = [0, -1]

    def al(arena, n):
        a = top[arena]
        top[arena] = a + (n + 15) // 16 * 16
        return (arena, a, a + n, 1, 128)

    def spans(v):
        if v[0] == "ind":
            return spans(v[1]) + spans(v[2])
        return [(v[0], v[1], v[2], v[3])]

    def add(eng, kind, args, rd, wr, busy, lat=0.0, sem=None, extra=()):
        r, w = [], []
        for v in rd:
            r += spans(v)
        for v in wr:
            if v[0] == "ind":
                w += spans(v[1])
                r += spans(v[2])
            else:
                w += spans(v)
        banks = sorted(set(s[0] for s in r + w if s[0].startswith("ps")))
        ops.append({"eng": eng, "kind": kind, "args": args, "r": r, "w": w, "busy": busy, "lat": lat, "sem": sem,
                    "banks": banks, "extra": list(extra), "chunk": now[0], "visit": now[1], "group": None, "slot": None})
        if now[1] >= 0:
            name, a, b, st = (w + r)[0] if kind != "dma" else r[0]
            for a0, b0, n in named.get(name, []):
                if a0 <= a < b0:
                    name, a = n, a - a0
                    break
            sig = (eng, name, a)
            seen[(now[0], now[1], sig)] = seen.get((now[0], now[1], sig), 0) + 1
            ops[-1]["slot"] = sig + (seen[(now[0], now[1], sig)],)
        return len(ops) - 1

    def narrow(vs):
        return all(v[0] in ("ba", "ha", "ua") for v in vs)

    def vcost(out, ins, per):
        if out[0] == "ind":
            return 0.05 + count(out) * SCY * CY
        if ins and ins[0][0] == "ind":
            return 0.05 + count(out) * GCY * CY
        return 0.03 + max(64, count(out) * per) * CY

    def tt(out, a, b, op):
        per = 1.0 if (a[0].startswith("ps") or b[0].startswith("ps")) else 2.0
        return add("V", "tt", (out, a, b, op), [a, b], [out], vcost(out, [a], per))

    def ts(out, a, s1, s2, op0, op1=None):
        rd = [a] + [s for s in (s1, s2) if isap(s)]
        return add("V", "ts", (out, a, s1, s2, op0, op1), rd, [out], vcost(out, [a], 0.5 if narrow([out, a]) else 1.0))

    def cp(out, a):
        return add("V", "cp", (out, a), [a], [out], vcost(out, [a], 0.5 if narrow([out, a]) else 1.0))

    def ms(out, c):
        return add("V", "ms", (out, c), [], [out], vcost(out, [], 0.5 if narrow([out]) else 1.0))

    def scan(out, d0, d1, op):
        return add("V", "scan", (out, d0, d1, op), [d0, d1], [out], vcost(out, [d0], 0.5 if narrow([out, d0, d1]) else 1.0))

    def act(out, a, func, bias=0.0, scale=1.0):
        rd = [a] + [s for s in (bias, scale) if isap(s)]
        return add("S", "act", (out, a, func, bias, scale), rd, [out],
                   0.065 + count(out) * (GCY if a[0] == "ind" else 1.0) * CY)

    def mm(lst, ends="se", after=()):
        key = lst[0][0][0]
        group = [] if "s" in ends else opened[key]
        busy = 0.03 + sum(max(64, count(m[2])) * (4 if m[2][0] == "fa" else 1) for m in lst) * PCY
        i = add("P", "mm", (lst, "s" in ends, "e" in ends), [m[1] for m in lst] + [m[2] for m in lst], [m[0] for m in lst],
                busy, 0.05, None, list(after) + (group if "e" in ends else group[:1]))
        opened[key] = group + [i]
        ops[i]["group"] = opened[key][0]
        return i

    def iota(out, pattern, base, cm):
        add("G", "iota", (out, pattern, base, cm), [], [out], 0.15 + 2 * count(out) * CY)

    def select(out, a, pattern, op, fill, base, cm):
        add("G", "sel", (out, a, pattern, op, fill, base, cm), [a], [out], 0.2 + 2 * count(out) * CY)

    def dma(eng, out, a, lat):
        s = "d%d" % len(sems)
        sems.append(s)
        add(eng, "dma", (out, a), [a] if a[0] != "hbm" else [], [out] if out[0] != "hbm" else [], 0.1, lat, s)

    def send(d, src, dst, lat, after=()):
        s = "r%d" % len(sems)
        sems.append(s)
        i = add("G", "send", [(d, src, dst, s)], [src], [], SEND, extra=after)
        add("R", "arrive", (d, s), [], [dst], 0.0, lat - HOP, s, [i])
        return i

    XW0 = al("ba", 16 + 4096)
    XW = sl(XW0, 16, 16 + 4096)
    QI, HI, GI, ZI, TI = al("ia", 1024), al("ia", 128), al("ia", 128), al("ia", 128), al("ia", 1)
    dma("S", HI, ("hbm", "hn"), 2.0)
    dma("Y", GI, ("hbm", "gt"), 2.0)
    dma("S", ZI, ("hbm", "zs"), 2.1)
    dma("Y", QI, ("hbm", "qs"), 3.0)
    dma("S", TI, ("hbm", "th"), 2.2)
    dma("Y", XW, ("hbm", "xt"), 5.5)

    AND, SHR = OP.bitwise_and, OP.arith_shift_right
    K = 2.0 ** 25
    i1, i2, i4, i5, i6 = al("ia", 128), al("ia", 128), al("ia", 144), al("ia", NV), al("ia", L // 8)
    iota(i1, [[-1, 128]], 256, 1)
    iota(i2, [[-16, 8], [0, 16]], 0, 1)
    iota(i5, [[-1, NV]], 16, 1)
    iota(i4, [[1, 144]], -14, 0)
    iota(i6, [[16, L // 8]], 0, 0)
    j1, j2, j5 = al("ia", 128), al("ia", 128), al("ia", NV)
    ONE, DM, tmpb = al("ba", 128), al("ba", 128), al("ba", 128)
    ts(j1, i1, 15, None, AND)
    ts(j2, i2, 4, None, SHR)
    ts(ONE, j2, 0.0, None, OP.is_equal)
    ts(tmpb, j2, 0.0, -64.0, OP.not_equal, OP.mult)
    tt(DM, j1, tmpb, OP.add)
    ts(j5, i5, 15, None, AND)
    KP, B1, G16, IO = al("fa", NV), al("fa", NV), al("fa", 1), al("fa", L // 8)
    cp(KP, j5)
    ts(B1, j5, -8192.0, 4096.0, OP.mult, OP.add)
    ts(IO, i6, sl(KP, 0, 1), None, OP.add)
    ts(G16, sl(i5, 0, 1), sl(KP, 0, 1), -16.0, OP.subtract, OP.add)
    SEL, DG, C14, t144 = al("ba", 144), al("ba", 144), al("ba", 144), al("ba", 144)
    ts(C14, i4, G16, None, OP.subtract)
    ts(SEL, C14, 1.0, -K, OP.is_equal, OP.mult)
    ts(t144, C14, 0.5, None, OP.subtract)
    act(t144, t144, AF.Abs)
    ts(DG, t144, 1.0, float(2 * L), OP.is_lt, OP.mult)

    def mat(arena, d, w):
        m = al(arena, 128)
        ts(m, DM, float(d), float(w), OP.is_equal, OP.mult)
        return m

    def scaled(arena, src, w):
        m = al(arena, 128)
        act(m, src, AF.Identity, 0.0, float(w))
        return m

    I, R5, R1, R4, R11 = mat("ba", 0, 1), mat("ba", 5, 1), mat("ba", 15, 1), mat("ba", 4, 1), mat("ba", 11, 4096)
    Ia, Ib, nI, Ih = mat("ba", 0, 2080), mat("ba", 0, 3232), mat("ba", 0, -1), mat("ba", 0, 0.5)
    R5a, R5b, nR5, R1a = scaled("ba", R5, 2080), scaled("ba", R5, 3232), scaled("ba", R5, -1), scaled("ba", R1, 2080)
    IK, nIK, I32, nONEK = scaled("ba", I, K), scaled("ba", I, -K), scaled("ba", I, 32), scaled("ba", ONE, -K)
    ONE2k, nONE2k, ONE128 = scaled("ba", ONE, 2048), scaled("ba", ONE, -2048), scaled("ba", ONE, 128)
    ONEf, R5f, R1f = scaled("fa", ONE, 1), scaled("fa", R5, 1), scaled("fa", R1, 1)
    nR1w, nR5w, R10 = scaled("ba", R1, -8192), scaled("ba", R5, -8192), mat("ba", 10, 1)
    diag = [[-1, 128]]
    BK, BLK, LESS5 = mat("ba", 11, 4096), mat("ba", 5, -K * 2 ** 13), mat("ba", 5, -1)
    select(BK, BK, diag, OP.not_equal, -4096.0, 0, 1)
    select(BLK, BLK, diag, OP.not_equal, K * 2 ** 14, 0, 1)
    select(LESS5, LESS5, diag, OP.not_equal, 1.0, 0, 1)
    W = []
    for t in range(NV):
        m = al("ba", 128)
        ts(m, DM, sl(KP, t, t + 1), -8192.0, OP.is_gt, OP.mult)
        select(m, m, diag, OP.not_equal, 8192.0, 0, 1)
        W.append(m)
    ONES, EVEN, THIRD = al("ba", 2 * L), al("ba", 4 * L), al("ba", 3 * L)
    ms(ONES, 1.0)
    ms(rows(EVEN, 1), 0.0)
    ms(rows(sl(EVEN, 0, 4 * L, 2), 1), 1.0)
    ms(rows(THIRD, 3), 0.0)
    ms(rows(sl(THIRD, 2, 3 * L, 3), 3), 1.0)
    ms(rows(sl(THIRD, 2, 3 * L, 3), 1), 0.0)
    ms(rows(sl(THIRD, 0, 3 * L, 3), 1), 1.0)
    cb = {}

    def bias(out, cs, pattern=None):
        if cs not in cb:
            cb[cs] = al("ba", 128)
            keep = list(now)
            now[0], now[1] = 0, -1
            for k in range(len(cs), 0, -1):
                ms(rows(cb[cs], k), float(cs[k - 1]))
            now[0], now[1] = keep
        return (out, rows(cb[cs], len(cs)), rows(pattern or sl(ONES, 0, count(out)), len(cs)))

    ms(sl(XW0, 0, 16), 0.0)
    RS = al("ba", 8 * L)
    ms(RS, 1.0)
    ms(sl(RS, 0, 8 * L, 16), 0.0)

    ps = [("ps%d" % b, 0, 512, 1, 128) for b in range(8)]

    def region(c, name):
        b, k, n = (cfg["banks"][name] + (1,))[:3]
        return sl(ps[NB * c + b], k * L, (k + n) * L)

    TH, TB = al("fa", 16 * NV), [al("ha", L) for t in range(NV)]
    ts(sl(TH, 0, 1), TI, -2048.0, None, OP.add)
    for t in range(NV):
        act(TB[t], sl(ONES, 0, L), AF.Identity, sl(TH, 16 * t, 16 * t + 1), 0.0)
        if t < NV - 1:
            pT = sl(ps[7], 7 * L, 7 * L + 1)
            mm([(pT, R1f, sl(TH, 16 * t, 16 * t + 1))])
            act(sl(TH, 16 * t + 16, 16 * t + 17), pT, AF.Identity)

    ch = []
    for c in range(NCH):
        now[0] = c
        d = {"Q": al("fa", 8 * L), "QO": al("fa", 8 * L), "E3": al("fa", 3 * L), "S3": al("fa", 3 * L),
             "E4": al("ba", 4 * L), "RF1": al("ha", 4 * L), "RF": al("ha", 2 * L)}
        for n in ("lt", "st"):
            d[n] = [al("ha", 4 * L) for t in range(NV + 1)]
        for n in ("lb", "sb"):
            d[n] = [al("fa", 4 * L) for t in range(NV)]
        for n in ("lu", "su"):
            d[n] = [al("ua", L + L // 8) for t in range(NV + 1)]
        for n in ("d", "eq", "e", "tmp"):
            d[n] = al("fa", 2 * L)
        for n in ("t0", "t1", "J", "N0m", "x", "dm", "t2", "go", "zo"):
            d[n] = al("fa", L)
        for n in ("N0", "N1", "I0", "I1", "Ng", "G", "Nx"):
            d[n] = al("ia", L)
        d["w"], d["Ix"] = al("ia", L // 8), al("ia", L + L // 8)
        for n in ("X", "D", "AB", "SC"):
            d[n] = al("ba", 16 * L)
        d["m0"], d["r"], d["Fs"] = al("ba", L), al("ha", L), al("ha", L)
        for n in ("u0", "u1"):
            d[n] = al("ua", L)
        ch.append(d)
        for n in d:
            for v in (d[n] if isinstance(d[n], list) else [d[n]]):
                named.setdefault(v[0], []).append((v[1], v[2], n))
        for b in range(4):
            ts(sl(d["Q"], 2 * L * b, 2 * L * (b + 1)), sl(QI, 256 * b + 2 * L * c, 256 * b + 2 * L * (c + 1)),
               2048.0, None, OP.add)
        ms(sl(d["E3"], 0, 3 * L, 3), 0.0)
        ms(sl(d["E4"], 0, 4 * L, 2), 0.0)

    def xindex(c, Hc, r, ra, Gc):
        d = ch[c]
        pp, pk = region(c, "pp"), region(c, "pk")
        mm([bias(pp, (3232,)), (pp, r, Hc)])
        mm([(pk, ra, Hc)])
        tt(d["t2"], pp, Gc, OP.mult)
        tt(d["Nx"], pk, d["t2"], OP.add)
        ts(sl(d["Ix"], 0, L), d["Nx"], 5, 4095, SHR, AND)

    def callee(c, Z):
        d = ch[c]
        pc = sl(region(c, "pc"), 0, L // 8)
        mm([(pc, sl(DG, 14 - 2 * k, 142 - 2 * k), sl(Z, k, L, 8)) for k in range(8)])
        tt(d["w"], pc, IO, OP.add)
        ts(sl(d["Ix"], L, L + L // 8), d["w"], 8 * L - 1, None, AND)

    def update(c, t, Q):
        d = ch[c]
        win = ("ind", Q, sl(d["lu"][t - 1], L, L + L // 8))
        tt(d["tmp"], win, sl(d["lb"][t], 2 * L, 4 * L), OP.subtract)
        tt(win, d["tmp"], sl(d["lb"][t], 0, 2 * L), OP.max)

    def distance(c, pe, U, pieces, plain, terms):
        d = ch[c]
        for k, (a, b) in enumerate(cuts(pieces)):
            D, X = sl(d["D"], 16 * a, 16 * b), sl(d["X"], 16 * a, 16 * b)
            if k in plain:
                i = act(D, ("ind", XW, sl(U, a, b)), AF.Identity)
                diff = sl(region(c, "p4"), 0, 16 * (b - a))
                mm([(diff, I, D), (diff, nI, X)])
                D = diff
            else:
                i = tt(D, ("ind", XW, sl(U, a, b)), X, OP.subtract)
            if k == 0:
                mm([bias(pe, (2048 * K, 15.5 * K))] + [(pe, w, x) for w, x in terms], "s", [i])
            act(sl(d["AB"], 16 * a, 16 * b), D, AF.Abs)
        return mm([(pe, sl(SEL, 15 - p, 143 - p), sl(d["AB"], p, 16 * L, 16)) for p in range(16)], "e")

    for c in range(NCH):
        now[0] = c
        d = ch[c]
        f0 = d["lt"][0]
        ts(sl(f0, 0, L), sl(GI, L * c, L * c + L), -2048.0, None, OP.add)
        ts(sl(f0, L, 2 * L), sl(ZI, L * c, L * c + L), ZOFF, None, OP.add)
        ts(sl(f0, 2 * L, 3 * L), sl(ZI, L * c, L * c + L), 0.0, None, OP.is_ge)
        ts(sl(f0, 3 * L, 4 * L), sl(HI, L * c, L * c + L), -2048.0, None, OP.add)
        xindex(c, sl(f0, 3 * L, 4 * L), I, Ia, sl(f0, 0, L))
        callee(c, sl(f0, L, 2 * L))
        cp(d["lu"][0], d["Ix"])

    def visit(c, t):
        d = ch[c]
        pN0, pN, pe, pf, po, p4, p3, pF, pw, pwk, pzr, pz, pM, pb = [
            region(c, n) for n in "pN0 pN e0 pf0 po0 p4 p3 pF pw pwk pzr pz pM pb".split()]
        fa, fb = sl(pf, 0, L), sl(pf, L, 2 * L)
        U, LT, ST, SU = d["lu"][t], d["lt"][t], d["st"][t + 1], d["su"][t + 1]
        Gc, Z, UP, Hc = [sl(LT, k * L, k * L + L) for k in range(4)]
        Gn, Zn, un1, Hn = [sl(ST, k * L, k * L + L) for k in range(4)]
        RF, m0, e1, e2 = d["RF"], d["m0"], sl(d["e"], 0, L), sl(d["e"], L, 2 * L)
        R, F = sl(RF, 0, 2 * L, 2), sl(RF, 1, 2 * L, 2)
        RF1, Ra, Fa = sl(d["RF1"], 1, 4 * L, 2), sl(d["RF1"], 1, 4 * L, 4), sl(d["RF1"], 3, 4 * L, 4)
        last = t == NV - 1
        before = [(IK, TB[t]), (nONEK, UP)]
        if t > 1:
            update(c, t - 1, d["Q"])
        act(RF, ("ind", d["Q"], sl(U, L, L + L // 8)), AF.Identity, -4096.0)
        for k, (a, b) in enumerate(cuts(cfg["xp"])):
            if k in cfg["xonv"][c]:
                cp(sl(d["X"], 16 * a, 16 * b), ("ind", XW, sl(U, a, b)))
            else:
                act(sl(d["X"], 16 * a, 16 * b), ("ind", XW, sl(U, a, b)), AF.Identity)
        if last:
            act(d["QO"], d["Q"], AF.Identity, -2048.0)
        mm([(pN0, Ia, R), (pN0, Ib, F)])
        tt(d["t0"], R, F, OP.mult)
        tt(d["N0"], d["t0"], pN0, OP.add)
        ts(d["I0"], d["N0"], 5, 4095, SHR, AND)
        cp(d["u0"], d["I0"])
        sums = distance(c, pe, d["u0"], cfg["p0"], cfg["plain0"][c], before)
        mm([bias(pf, (0,)), (fa, I, R), (fb, I, Hc), (fb, nI, R)], "s", [sums])
        mark = act(m0, pe, AF.Sigmoid, 0.0, 2.0 ** -16)
        mm([(fa, W[t], m0), (fb, W[t], m0)], "e")
        tt(d["N0m"], d["N0"], pe, OP.min)
        mm([bias(po, (-4096,))], "s", [mark])
        mm([bias(p4, (-4096,), EVEN), (sl(p4, 1, 4 * L, 2), I, RF)], "s", [sums])
        act(d["e"], pf, AF.Relu, -4096.0)
        mm([(po, ONEf, e1)], "e")
        mm([(sl(p4, 0, 4 * L, 4), ONEf, e2), (sl(p4, 2, 4 * L, 4), ONEf, e2)], "e")
        tt(sl(d["E4"], 1, 4 * L, 4), R, po, OP.is_equal)
        tt(sl(d["E4"], 3, 4 * L, 4), F, po, OP.is_equal)
        scan(d["RF1"], d["E4"], p4, OP.add)
        tt(d["t1"], Ra, Fa, OP.mult)
        mm([(pN, R5a, Ra), (pN, R5b, Fa), (pN, nIK, m0)], "s")
        mm([(pN, R5f, d["t1"])], "e")
        tt(d["N1"], pN, d["N0m"], OP.max)
        ts(d["I1"], d["N1"], 5, 4095, SHR, AND)
        cp(d["u1"], d["I1"])
        raf, rd, nrw = (R5f, R10, nR5w) if last else (R1f, R4, nR1w)
        mm([(pF, LESS5, Fa)])
        tt(d["x"], pF, m0, OP.mult)
        mm([(pF, rd, Fa), (pF, raf, d["x"])])
        act(d["Fs"], pF, AF.Identity)
        pe, pf, po = region(c, "e1"), region(c, "pf1"), region(c, "po1")
        fa, fb = sl(pf, 0, L), sl(pf, L, 2 * L)
        sums = distance(c, pe, d["u1"], cfg["p1"], cfg["plain1"][c], before + [(BLK, m0)])
        mm([bias(pf, (0,)), (fa, nR5, Ra), (fa, W[t], m0), (fb, nI, Hc), (fb, R5, Ra), (fb, W[t], m0)], "s", [sums])
        mark = act(un1, pe, AF.Sigmoid, 0.0, -2.0 ** -16)
        mm([(fa, W[t], un1), (fb, W[t], un1)], "e")
        mm([bias(po, (-4096,))], "s", [mark])
        mm([bias(p3, (-4096, -896 * 2 ** 16, 2 ** 16), THIRD), (sl(p3, 1, 3 * L, 3), I, d["Fs"]),
            (sl(p3, 2, 3 * L, 3), ONE2k, Z)], "s", [sums])
        act(d["e"], pf, AF.Relu, sl(B1, t, t + 1), -1.0)
        mm([(po, ONEf, e1)], "e")
        tt(d["J"], d["I1"], pe, OP.min)
        ts(d["u0"], d["J"], 16.0, 0.0, OP.add, OP.max)
        for k, (a, b) in enumerate(cuts(cfg["ps"])):
            Y, src = sl(d["AB"], 16 * a, 16 * b), ("ind", XW0, sl(d["u0"], a, b))
            if k in cfg["onv"][c]:
                ts(Y, src, 0.5, None, OP.mult)
            else:
                act(Y, src, AF.Identity, 0.0, 0.5)
            scan(sl(d["SC"], 16 * a, 16 * b), sl(RS, 0, 16 * (b - a)), Y, OP.max)
        mm([(pzr, Ih, Z), (pzr, ONE128, un1)])
        act(d["r"], pzr, AF.Relu, 0.25 - ZOFF / 2 - 2048.0)
        mm([bias(pz, (ZOFF / 2, -0.25)), (pz, Ih, Z), (pz, I, d["r"])])
        tt(Zn, sl(d["SC"], 15, 16 * L, 16), pz, OP.add)
        mm([(pwk, ONE, Z), (pwk, nrw, un1)])
        act(sl(d["E3"], 2, 3 * L, 3), pwk, AF.Relu, 32.0 - 16 * ZOFF)
        mm([bias(pw, (3 * 2 ** 24,)), (pw, nONE2k, Z), (pw, I32, Gc)])
        tt(d["dm"], pw, un1, OP.mult)
        mm([(sl(p3, 2, 3 * L, 3), raf, d["dm"])], "")
        mm([(sl(p3, 0, 3 * L, 3), ONEf, e2)], "e")
        tt(sl(d["E3"], 1, 3 * L, 3), d["Fs"], po, OP.is_equal)
        scan(d["S3"], d["E3"], p3, OP.add)
        cp(d["Ng"], sl(d["S3"], 2, 3 * L, 3))
        ts(d["G"], d["Ng"], 5, 4095, SHR, AND)
        if t > 0:
            for h in range(2):
                mm([(sl(pM, h, 2 * L, 2), R11, un1), (sl(pM, h, 2 * L, 2), BK, m0)])
            act(sl(d["sb"][t], 2 * L, 4 * L), pM, AF.Identity)
            mm(([bias(pb, (-2048,))] if last else []) + [(pb, I, RF1)] +
               [(sl(pb, h, 2 * L, 2), w, x) for h in range(2) for w, x in ((R11, un1), (BK, m0))])
            for h, x in enumerate((Ra, Fa)):
                tt(sl(d["eq"], h, 2 * L, 2), x, po, OP.is_equal)
            for h in range(2):
                tt(sl(d["d"], h, 2 * L, 2), sl(d["eq"], h, 2 * L, 2), sl(p3, 0, 3 * L, 3), OP.mult)
            tt(sl(d["sb"][t], 0, 2 * L), pb, d["d"], OP.add)
            send("b", d["sb"][t], d["lb"][t], 2.7)
        if last:
            cp(d["go"], d["G"])
            act(d["zo"], Zn, AF.Identity, -ZOFF)
            dma("Y", ("hbm", "yg", L * c, L * c + L), d["go"], 2.0)
            dma("Y", ("hbm", "yz", L * c, L * c + L), d["zo"], 2.0)
            update(c, t, d["QO"])
            for b in range(4):
                dma("YS"[b % 2], ("hbm", "yq", 256 * b + 2 * L * c, 256 * b + 2 * L * (c + 1)),
                    sl(d["QO"], 2 * L * b, 2 * L * (b + 1)), 2.2)
        else:
            mm([(region(c, "pH"), R1, Hc)])
            act(Hn, region(c, "pH"), AF.Identity)
            ts(Gn, d["G"], -2048.0, None, OP.add)
            xindex(c, Hc, R1, R1a, Gn)
            callee(c, Zn)
            lists = []
            for a, b in (((L, L + L // 8), (0, L)) if cfg["split"] else ((0, L + L // 8),)):
                cp(sl(SU, a, b), sl(d["Ix"], a, b))
                lists.append(send("f", sl(SU, a, b), sl(d["lu"][t + 1], a, b), 2.2))
            send("f", ST, d["lt"][t + 1], 2.4, lists)

    for t in range(NV):
        now[1] = t
        for c in range(NCH):
            now[0] = c
            visit(c, t)
    return ops, sems, top


def depend(ops):
    hist = {}
    for i, o in enumerate(ops):
        hard, soft = set(), set(o["extra"])
        if o["eng"] == "R":
            hard, soft = soft, hard
        for kind, sp in (("r", o["r"]), ("w", o["w"])):
            for name, a, b, st in sp:
                for j, k2, a2, b2, st2 in hist.get(name, []):
                    if j != i and a < b2 and a2 < b and (kind == "w" or k2 == "w") and (a - a2) % math.gcd(st, st2) == 0:
                        (soft if ops[j]["eng"] == "P" and o["eng"] == "P" else hard).add(j)
        for name, a, b, st in o["w"]:
            hist[name] = [h for h in hist.get(name, [])
                          if not (a <= h[2] and h[3] <= b and (st == 1 or (st == h[4] and (a - h[2]) % st == 0)))]
        for kind, sp in (("r", o["r"]), ("w", o["w"])):
            for name, a, b, st in sp:
                hist.setdefault(name, []).append((i, kind, a, b, st))
        o["data"], o["soft"] = hard, soft - hard


def label(o):
    if o["slot"] is None:
        return None
    e, name, a, k = o["slot"]
    if name.startswith("ps"):
        name = "bank%d" % (int(name[2]) % NB)
    return "%s %s %d %d" % (e, name, a, k)


def schedule(ops, lead, look, shift):
    n = len(ops)
    succ, left = [[] for i in range(n)], [0] * n
    for i, o in enumerate(ops):
        for j in o["data"] | o["soft"]:
            succ[j].append(i)
            left[i] += 1
    prio, bulk = [0.0] * n, {}
    for i in range(n - 1, -1, -1):
        o = ops[i]
        best = o["lat"]
        for s in succ[i]:
            best = max(best, prio[s] + (o["lat"] + HOP if i in ops[s]["data"] else 0.0))
        if o["busy"] > 0.3 and o["eng"] in "VS":
            kind = (o["eng"], o["chunk"], o["visit"])
            best = max(best, bulk.get(kind, 0.0))
            bulk[kind] = best + o["busy"]
        prio[i] = best + o["busy"]
    for i in range(n):
        prio[i] += (lead if ops[i]["chunk"] == 0 else 0.0) + shift.get(label(ops[i]), 0.0)
    free, bank, done, held, due, taken = {}, {}, [0.0] * n, {}, [0.0] * n, []
    ready = [i for i in range(n) if left[i] == 0]

    def start(i):
        o = ops[i]
        s = max(due[i], free.get(o["eng"], 0.0) if o["eng"] != "R" else 0.0)
        for b in o["banks"]:
            for e, j in bank.get(b, {}).items():
                if e != o["eng"]:
                    s = max(s, done[j] + HOP)
        return s

    while ready:
        st = [(start(i), i) for i in ready
              if ops[i]["eng"] != "P" or held.get(ops[i]["banks"][0]) in (None, ops[i]["group"])]
        s0, i0 = min(st)
        cand = [(prio[i], -i, s) for s, i in st if ops[i]["eng"] == ops[i0]["eng"] and s <= s0 + look * ops[i0]["busy"]]
        p, i, s = max(cand)
        i = -i
        o = ops[i]
        for b in o["banks"]:
            bank.setdefault(b, {})[o["eng"]] = i
            if o["group"] is not None:
                held[b] = None if o["args"][2] else o["group"]
        o["start"], o["turn"] = s, len(taken)
        taken.append(i)
        free[o["eng"]] = s + o["busy"]
        done[i] = s + o["busy"] + o["lat"]
        ready.remove(i)
        for k in succ[i]:
            due[k] = max(due[k], done[i] + HOP if i in ops[k]["data"] else s)
            left[k] -= 1
            if left[k] == 0:
                ready.append(k)
    return max(done)


def repeat(ops):
    n = len(ops)
    slot = {(o["slot"], o["chunk"]): o["start"] + 1e-7 * i for i, o in enumerate(ops) if o["visit"] == 2}
    firsts = [min(o["start"] for o in ops if o["visit"] == t and o["kind"] == "send") for t in (2, 3)]
    beat = firsts[1] - firsts[0]
    key = [slot[(o["slot"], o["chunk"])] + beat * (o["visit"] - 2) if (o["slot"], o["chunk"]) in slot else None for o in ops]
    late = [1e9] * n
    for i in range(n - 1, -1, -1):
        if key[i] is None and late[i] < 1e9:
            key[i] = late[i] - ops[i]["busy"] - ops[i]["lat"] - HOP
        for j in ops[i]["data"] | ops[i]["soft"]:
            late[j] = min(late[j], 1e9 if key[i] is None else key[i])
    succ, left = [[] for i in range(n)], [0] * n
    for i, o in enumerate(ops):
        if key[i] is None:
            key[i] = max([key[j] + ops[j]["busy"] + ops[j]["lat"] for j in o["data"] | o["soft"]] + [0.0])
        for j in o["data"] | o["soft"]:
            succ[j].append(i)
            left[i] += 1
    ready, held, now = [i for i in range(n) if left[i] == 0], {}, -1e9
    while ready:
        i = min((key[i], i) for i in ready
                if ops[i]["group"] is None or held.get(ops[i]["banks"][0]) in (None, ops[i]["group"]))[1]
        ready.remove(i)
        key[i] = now = max(key[i], now + 1e-7)
        if ops[i]["group"] is not None:
            held[ops[i]["banks"][0]] = None if ops[i]["args"][2] else ops[i]["group"]
        for j in succ[i]:
            left[j] -= 1
            if left[j] == 0:
                ready.append(j)
    return key, beat, slot


def improve(ops, key, beat, slot, tries, heat, seed):
    n = len(ops)
    names, var, shift, phase = {}, [], [], []
    for i, o in enumerate(ops):
        name = (o["slot"], o["chunk"]) if 0 < o["visit"] < NV - 1 and (o["slot"], o["chunk"]) in slot else i
        shift.append(beat * max(o["visit"], 0))
        if name not in names:
            names[name] = len(phase)
            phase.append(key[i] - shift[i])
        var.append(names[name])
    up, down, info = {}, {}, []
    for i, o in enumerate(ops):
        for j in sorted(o["data"] | o["soft"]):
            if var[i] != var[j]:
                up.setdefault(var[i], {})[(var[j], shift[i] - shift[j])] = 1
                down.setdefault(var[j], {})[(var[i], shift[i] - shift[j])] = 1
        pre = [(j, ops[j]["lat"] + HOP) for j in o["data"]] + [(j, 0.0) for j in o["soft"]]
        info.append((pre, "VSPGYR".index(o["eng"]), o["busy"], [int(b[2]) for b in o["banks"]], o["lat"] + HOP, o["group"],
                     None if o["group"] is None or o["args"][2] else o["group"]))
    state = [seed]

    def draw():
        state[0] = (state[0] * 1103515245 + 12345) % 2 ** 31
        return state[0] / 2 ** 31

    def run(ph):
        end, why, ready = [None] * n, [-1] * n, [0.0] * n
        last, held, bank = [-1] * 6, [None] * 8, [[-1, -1, -1] for b in range(8)]
        for x, i in sorted((ph[var[i]] + shift[i], i) for i in range(n)):
            pre, e, busy, banks, tail, group, keeps = info[i]
            s, w = 0.0, -1
            for j, gap in pre:
                x = end[j]
                if x is None:
                    return None
                if x + gap > s:
                    s, w = x + gap, j
            ready[i] = s
            if e < 5:
                p = last[e]
                if p >= 0 and end[p] > s:
                    s, w = end[p], p + n
                last[e] = i
            for b in banks:
                m = bank[b]
                for e2 in (0, 1, 2):
                    p = m[e2]
                    if e2 != e and p >= 0 and end[p] + info[p][4] > s:
                        s, w = end[p] + info[p][4], p + n
                m[e] = i
                if e == 2:
                    if held[b] is not None and held[b] != group:
                        return None
                    held[b] = keeps
            end[i], why[i] = s + busy, w
        return max(end[i] + info[i][4] for i in range(n)) + 0.3 * sum(end) / n, end, why, ready

    def waits(r):
        end, why = r[1], r[2]
        x = max((end[i] + info[i][4], i) for i in range(n))[1]
        path = []
        while why[x] >= 0:
            if why[x] >= n and var[why[x] - n] != var[x]:
                path.append((why[x] - n, x))
            x = why[x] % n
        return path, [(w - n, i) for i, w in enumerate(why) if w >= n and var[w - n] != var[i]]

    def move(ph, v, to, side, sign):
        ph[v] = to
        for u, d in side.get(v, ()):
            if sign * (ph[u] - (to + sign * d)) >= 0:
                move(ph, u, to + sign * d - sign * 1e-6 * (1 + draw()), side, sign)

    cur = run(phase)
    if cur is None:
        return key
    path, more = waits(cur)
    best = (cur[0], list(phase))
    for t in range(tries):
        pick = path if draw() < 0.8 and path else more
        p, x = pick[int(draw() * len(pick))]
        new, kind = list(phase), draw()
        if kind < 0.3:
            late = cur[3][x] + 0.3 * draw() - 0.1
            p = min((cur[1][q], q) for q in range(n) if info[q][1] == info[x][1] and cur[1][q] - info[q][2] >= late or q == x)[1]
            if var[p] == var[x]:
                continue
        d = shift[x] - shift[p]
        if kind < 0.65:
            move(new, var[x], phase[var[p]] - d - 1e-5 * (1 + draw()), up, 1)
        else:
            move(new, var[p], phase[var[x]] + d + 1e-5 * (1 + draw()), down, -1)
        r = run(new)
        if r is not None and r[0] <= cur[0] + heat * draw() ** 3 * (1 - t / tries):
            phase, cur = new, r
            path, more = waits(cur)
            if r[0] < best[0]:
                best = (r[0], list(phase))
    return [best[1][var[i]] + shift[i] for i in range(n)]


def finish(ops, key):
    order = [i for x, i in sorted((key[i], i) for i in range(len(ops)))]
    done, free, bank, need, cnt = {}, {}, {}, set(), {}
    known = {}
    for k, i in enumerate(order):
        o = ops[i]
        hard = set(o["data"])
        for b in o["banks"]:
            hard |= set(j for e, j in bank.get(b, {}).items() if e != o["eng"])
            bank.setdefault(b, {})[o["eng"]] = i
        o["start"] = max([free.get(o["eng"], 0.0) if o["eng"] != "R" else 0.0] + [done[j] + HOP for j in hard])
        free[o["eng"]] = o["start"] + o["busy"]
        done[i] = o["start"] + o["busy"] + o["lat"]
        o["place"], o["hard"] = k, set()
        mine = known.setdefault(o["eng"], {})
        for x, j in sorted(((ops[j]["place"], j) for j in hard), reverse=True):
            p = ops[j]
            if p["sem"] is not None or o["eng"] == "R":
                o["hard"].add(j)
            elif mine.get(p["eng"], -1) < x:
                o["hard"].add(j)
                mine[p["eng"]] = x
                for e in p["knows"]:
                    mine[e] = max(mine.get(e, -1), p["knows"][e])
        o["knows"] = dict(mine)
        need |= o["hard"]
    for i in order:
        o = ops[i]
        o["inc"] = None
        if o["sem"] is None and o["kind"] != "send" and i in need:
            cnt[o["eng"]] = cnt.get(o["eng"], 0) + 1
            o["inc"] = cnt[o["eng"]]
    return order, cnt, max(done.values())


def plan(cfg):
    ops, sems, top = build(cfg)
    depend(ops)
    schedule(ops, cfg["lead"], cfg["look"], cfg["shift"])
    key = [o["start"] + 1e-7 * o["turn"] for o in ops]
    key = [i - 1e6 if o["kind"] == "dma" and o["visit"] < 0 else key[i] for i, o in enumerate(ops)]
    return (ops, sems, top) + finish(ops, key)


OPS, SEMS, TOP, ORDER, TOTAL, SPAN = plan(CFG)

SCRATCH = {"fa": ("sbuf", [128, TOP["fa"]], "float32"), "ba": ("sbuf", [128, TOP["ba"]], "bfloat16"),
           "ha": ("sbuf", [128, TOP["ha"]], "float16"), "ia": ("sbuf", [128, TOP["ia"]], "int32"),
           "ua": ("sbuf", [128, TOP["ua"]], "uint16")}
for _b in range(8):
    SCRATCH["ps%d" % _b] = ("psum", [128, 512], "float32")
SEMAPHORES = ["qV", "qS", "qP", "qG", "sent"] + SEMS


def engines_of(T, topo, r):
    n = len(T.cores)
    e = {"f": topo.engines(T.cores[r], T.cores[(r + 1) % n]), "b": topo.engines(T.cores[r], T.cores[(r - 1) % n])}
    small, large = ("f", "b") if len(e["f"]) <= len(e["b"]) else ("b", "f")
    rest = [x for x in e[large] if x not in e[small]]
    if not rest:
        h = len(e[small]) // 2
        e[small], rest = e[small][:h], e[small][h:]
    e[large] = rest
    for k in e:
        m = 1
        while 2 * m <= len(e[k]):
            m *= 2
        e[k] = e[k][:m]
    return e


def rank_program(g, core, T, topo):
    r = T.rank_of(core)
    if r is None:
        return
    n = len(T.cores)
    mine = engines_of(T, topo, r)
    dest = {"f": T.cores[(r + 1) % n], "b": T.cores[(r - 1) % n]}
    comes = {"f": len(engines_of(T, topo, (r - 1) % n)["f"]), "b": len(engines_of(T, topo, (r + 1) % n)["b"])}
    queue = {"V": g.vector, "S": g.scalar, "P": g.tensor, "G": g, "Y": g.sync}
    seen = {e: {} for e in queue}
    final = {}
    sent = [0]

    def ap(v):
        if not isap(v):
            return v
        if v[0] == "ind":
            return ap(v[1]).indirect(ap(v[2]))
        if v[0] == "hbm":
            return T[v[1]][:] if len(v) == 2 else T[v[1]][:, v[2]:v[3]]
        cols = slice(v[1], v[2]) if v[3] == 1 else slice(v[1], v[2], v[3])
        return T[v[0]][:, cols] if v[4] == 128 else T[v[0]][0:v[4], cols]

    def mask(d):
        return sum(1 << e for e in mine[d])

    for i in ORDER:
        o = OPS[i]
        e, k, a = o["eng"], o["kind"], o["args"]
        if e == "R":
            final[a[1]] = comes[a[0]]
            continue
        q = queue[e]
        want = {}
        for j in o["hard"]:
            p = OPS[j]
            if p["eng"] == "R":
                s, v = p["sem"], comes[p["args"][0]]
            elif p["kind"] == "dma":
                s, v = p["sem"], 16
            else:
                s, v = "q" + p["eng"], p["inc"]
            want[s] = max(want.get(s, 0), v)
        for s in sorted(want):
            if seen[e].get(s, 0) < want[s]:
                q.wait_ge(T.sem[s], want[s])
                seen[e][s] = want[s]
        if k == "tt":
            ins = q.tensor_tensor(ap(a[0]), ap(a[1]), ap(a[2]), a[3])
        elif k == "ts":
            if a[5] is None:
                ins = q.tensor_scalar(ap(a[0]), ap(a[1]), ap(a[2]), None, a[4])
            else:
                ins = q.tensor_scalar(ap(a[0]), ap(a[1]), ap(a[2]), ap(a[3]), a[4], a[5])
        elif k == "cp":
            ins = q.tensor_copy(ap(a[0]), ap(a[1]))
        elif k == "ms":
            ins = q.memset(ap(a[0]), a[1])
        elif k == "scan":
            ins = q.tensor_tensor_scan(ap(a[0]), ap(a[1]), ap(a[2]), 0.0, OP.mult, a[3])
        elif k == "act":
            ins = q.activation(ap(a[0]), ap(a[1]), a[2], bias=ap(a[3]), scale=ap(a[4]))
        elif k == "iota":
            ins = q.iota(ap(a[0]), a[1], a[2], a[3])
        elif k == "sel":
            ins = q.affine_select(ap(a[0]), ap(a[1]), a[2], a[3], a[4], a[5], a[6])
        elif k == "mm":
            for m, (x, w, y) in enumerate(a[0]):
                ins = q.matmul(ap(x), ap(w), ap(y), a[1] and m == 0, a[2] and m == len(a[0]) - 1)
        elif k == "dma":
            q.dma_start(ap(a[0]), ap(a[1])).then_inc(T.sem[o["sem"]], 16)
            final[o["sem"]] = 16
            continue
        else:
            d, src, dst, s = a[0]
            rid, pid, se = topo.addr(dest[d])
            g.remote_dma(ap(dst), ap(src), T.sem[s], T.sem.sent, pid, rid, mask(d))
            sent[0] += len(mine[d])
            continue
        if o["inc"] is not None:
            ins.then_inc(T.sem["q" + e], 1)
    for e in TOTAL:
        final["q" + e] = TOTAL[e]
    final["sent"] = sent[0]
    for s in final:
        g.wait_ge(T.sem[s], final[s])
